import numpy as np
import ml_dtypes


def mxq(x, axis, fmt="e4m3"):
    dtype, down = {"e4m3": (ml_dtypes.float8_e4m3fn, 7), "e5m2": (ml_dtypes.float8_e5m2, 14)}[fmt]
    v = np.moveaxis(np.asarray(x, np.float32).astype(ml_dtypes.bfloat16).astype(np.float64), axis, -1)
    blocks = v.reshape(v.shape[:-1] + (-1, 32))
    amax = np.abs(blocks).max(-1, keepdims=True)
    byte = np.maximum(np.where(amax > 0, np.frexp(amax)[1] - 1 + 127, 0) - down, 1)
    scale = np.exp2(byte - 127.0)
    codes = (blocks / scale).astype(np.float32).astype(dtype).astype(np.float64)
    return np.moveaxis((codes * scale).reshape(v.shape), -1, axis)


WIDE = False


def mx_kscale(k):
    if not WIDE:
        return np.ones(k)
    levels = np.array([24, -24, 12, -12, 0])
    if k % 512:
        return np.exp2(np.random.permutation(np.resize(levels, k // 32))).repeat(32)
    a = np.empty((k // 512, 16))
    for p in range(k // 512):
        a[p, :8] = np.random.permutation(np.resize(levels, 8))
        for g in range(8):
            far = levels[np.abs(levels - a[p, g]) >= 10]
            a[p, g + 8] = far[np.random.randint(len(far))]
    return np.exp2(a.ravel()).repeat(32)


def f64(x):
    return np.asarray(x).astype(np.float64)


def striped(idx):
    return np.tile(idx.reshape(-1, 16).T, (8, 1)).astype(np.uint16)


def unstriped(offs):
    return offs[:16].T.reshape(-1).astype(np.int64)


E2M1 = np.array([0.0, 0.5, 1.0, 1.5, 2.0, 3.0, 4.0, 6.0, -0.0, -0.5, -1.0, -1.5, -2.0, -3.0, -4.0, -6.0])


def pack_weight(w, fmt):
    k, n = w.shape
    w = f64(np.asarray(w, np.float32).astype(ml_dtypes.bfloat16)).reshape(k // 32, 32, n)
    amax = np.abs(w).max(1)
    if fmt == "e4m3":
        byte = np.frexp(amax)[1] - 1 + 127 - 7
    else:
        mant, ex = np.frexp(amax / 6.0)
        byte = np.where(mant > 0.5, ex, ex - 1) + 127
    byte = np.clip(np.where(amax > 0, byte, 1), 1, 254)
    scaled = (w * np.exp2(127.0 - byte)[:, None, :]).reshape(k, n).astype(np.float32)
    by_word = np.ascontiguousarray(scaled.reshape(k // 512, 128, 4, n).transpose(0, 1, 3, 2))
    if fmt == "e4m3":
        words = by_word.astype(ml_dtypes.float8_e4m3fn).view(np.uint8)
    else:
        c = by_word.astype(ml_dtypes.float4_e2m1fn).view(np.uint8) & 0xF
        words = (c[..., 0::2] | (c[..., 1::2] << 4)).reshape(k // 512, 128, 2 * n)
    return np.ascontiguousarray(words), np.ascontiguousarray(byte.astype(np.uint8).reshape(k // 512, 16, n))


def unpack_weight(words, scales, fmt):
    g, _, n = scales.shape
    words = np.ascontiguousarray(words).reshape(g, 128, n, -1)
    if fmt == "e4m3":
        vals = words.view(ml_dtypes.float8_e4m3fn).astype(np.float64)
    else:
        nib = np.empty((g, 128, n, 4), np.uint8)
        nib[..., 0::2] = words & 0xF
        nib[..., 1::2] = words >> 4
        vals = E2M1[nib]
    vals = vals * np.repeat(np.exp2(scales.astype(np.float64) - 127.0), 8, axis=1)[..., None]
    return vals.transpose(0, 1, 3, 2).reshape(g * 512, n)


def pack_table4(v):
    words, scales = pack_weight(v, "e2m1")
    g, t = words.shape[0] // 2, v.shape[1]
    return np.ascontiguousarray(words.reshape(g, 2, 128, t, 2).transpose(0, 2, 3, 1, 4).reshape(g, 128, t, 4)), scales


def unpack_table4(words, scales):
    g, _, t, _ = words.shape
    return unpack_weight(words.reshape(g, 128, t, 2, 2).transpose(0, 3, 1, 2, 4).reshape(2 * g, 128, 2 * t), scales, "e2m1")


def sigm(f):
    return 1.0 / (1.0 + np.exp(-np.maximum(f, -700.0)))


K, L, N, T, J = 512, 1024, 512, 2048, 1024


def setup_inputs():
    n = np.random.standard_normal
    s = mx_kscale(K)[:, None]
    s2 = mx_kscale(L)[:, None]
    p_tab = pack_weight(n((K, T)) * s, "e4m3")
    p_tab2 = pack_table4(n((L, T)) * s2)
    p_zv = pack_weight(n((K, N)) / np.sqrt(K) / s, "e4m3")
    p_zt = pack_weight(n((L, N)) / np.sqrt(L) / s2, "e2m1")
    p_wv = pack_weight(n((K, N)) / np.sqrt(K) / s, "e4m3")
    return {
        "tab_words": p_tab[0],
        "tab_scales": p_tab[1],
        "tab2_words": p_tab2[0],
        "tab2_scales": p_tab2[1],
        "zv_words": p_zv[0],
        "zv_scales": p_zv[1],
        "zt_words": p_zt[0],
        "zt_scales": p_zt[1],
        "b": (0.3 * n(N)).astype(np.float32),
        "wv_words": p_wv[0],
        "wv_scales": p_wv[1],
        "wt": (n((L, N)) / np.sqrt(L) / s2).astype(np.float32),
        "offs": striped(np.random.permutation(T)[:J]),
        "offs2": striped(np.random.permutation(T)[:J]),
    }


def reference(tab_words, tab_scales, tab2_words, tab2_scales, zv_words, zv_scales, zt_words, zt_scales, b, wv_words, wv_scales, wt, offs, offs2):
    idx = unstriped(offs)
    idx2 = unstriped(offs2)
    tab_ = unpack_weight(tab_words, tab_scales, "e4m3")[:, idx]
    tab2_ = unpack_table4(tab2_words, tab2_scales)[:, idx2]
    zv_ = unpack_weight(zv_words, zv_scales, "e4m3")
    zt_ = unpack_weight(zt_words, zt_scales, "e2m1")
    z = zv_.T @ tab_ + zt_.T @ tab2_
    gate = sigm(z + f64(b)[:, None])
    wv_ = unpack_weight(wv_words, wv_scales, "e4m3")
    wt_ = mxq(f64(wt), 0, "e4m3")
    hv = wv_.T @ tab_
    ht = wt_.T @ tab2_
    av = np.tanh(hv)
    at = np.tanh(ht)
    return at + gate * (av - at)

@@ -1,0 +1,239 @@
+from contextlib import ExitStack
+
+import concourse.mybir as mybir
+
+K, L, N, T, J = 512, 1024, 512, 2048, 1024
+FLOPS = 2 * 2 * (K + L) * N * J
+
+F32 = mybir.dt.float32
+BF16 = mybir.dt.bfloat16
+I32 = mybir.dt.int32
+U32 = mybir.dt.uint32
+U16 = mybir.dt.uint16
+U8 = mybir.dt.uint8
+FP8X4 = mybir.dt.float8_e4m3fn_x4
+FP4X4 = mybir.dt.float4_e2m1fn_x4
+ALU = mybir.AluOpType
+TANH = mybir.ActivationFunctionType.Tanh
+
+P = 128
+PACK = 4
+QUADS = 4
+ROWS = 4
+M = 128
+N_TILES = N // M
+JC = 512
+J_CHUNKS = J // JC
+NH = 256
+
+
+def tile_list_gmu_tanh_none_kernel(
+    tc, tab_words, tab_scales, tab2_words, tab2_scales, zv_words, zv_scales, zt_words, zt_scales, b,
+    wv_words, wv_scales, wt, offs, offs2, out
+):
+    nc = tc.nc
+    with ExitStack() as ctx:
+        keep = ctx.enter_context(tc.tile_pool(name="keep", bufs=1))
+        work = ctx.enter_context(tc.tile_pool(name="work", bufs=3))
+        psum = ctx.enter_context(tc.psum_pool(name="psum", bufs=1))
+
+        def held(name, shape, dtype):
+            return keep.tile(shape, dtype, name=name, align_bytes=64)
+
+        list1 = keep.tile([P, J // 16], U16, name="list1")
+        list2 = keep.tile([P, J // 16], U16, name="list2")
+        s1_win = held("s1_win", [P, T // 4], I32)
+        s2_win = held("s2_win", [P, T // 4], I32)
+        s1_got = held("s1_got", [P, J // 4], I32)
+        s2_got = held("s2_got", [P, J // 4], I32)
+        v_plane = held("v_plane", [P, J // 4], I32)
+        t_planes = held("t_planes", [P, 2, J // 4], I32)
+        w_planes = held("w_planes", [P, 4, N // 4], I32)
+        w1_win = held("w1_win", [P, T], I32)
+        wv_sb = held("wv_sb", [P, N], I32)
+        zv_sb = held("zv_sb", [P, N], I32)
+        zt_sb = held("zt_sb", [P, 2, N // 2], I32)
+        w2_win = held("w2_win", [P, T], I32)
+        b_sb = held("b_sb", [P, N_TILES], F32)
+        half_b = held("half_b", [P, N_TILES], F32)
+        wt_codes = held("wt_codes", [P, 2, N], U32)
+        wt_plane = held("wt_plane", [P, 2, N], U8)
+        pieces = [(a, h) for h in range(N // NH) for a in range(2)]
+        wt_raw, wt_bf = {}, {}
+        v_got = [held("v_got%d" % c, [P, JC], U32) for c in range(J_CHUNKS)]
+        t_got = [held("t_got%d" % c, [P, JC], U32) for c in range(J_CHUNKS)]
+        t_part = [held("t_part%d" % c, [P, 2, 2 * JC], U8) for c in range(J_CHUNKS)]
+
+        nc.vector.memset(s2_win[:], 0)
+        nc.vector.memset(s1_win[:], 0)
+        nc.gpsimd.memset(w_planes[:], 0)
+
+        def load_wt(k):
+            a, h = k
+            wt_raw[k] = held("wt_raw%d%d" % k, [P, PACK, NH], F32)
+            rows = wt[512 * a : 512 * (a + 1), NH * h : NH * (h + 1)]
+            nc.sync.dma_start(out=wt_raw[k][:], in_=rows.rearrange("(p i) n -> p i n", i=PACK))
+
+        def words(ap):
+            return ap[0].rearrange("p n i -> p (n i)").bitcast(I32)
+
+        def cast(k):
+            wt_bf[k] = held("wt_bf%d%d" % k, [P, NH, PACK], BF16)
+            nc.scalar.copy(
+                out=wt_bf[k][:].rearrange("p (c n) i -> p c i n", n=4),
+                in_=wt_raw[k][:].rearrange("p i (c n) -> p c i n", n=4),
+            )
+
+        def quantise(k):
+            a, h = k
+            cols = slice(NH * h, NH * (h + 1))
+            nc.vector.quantize_mx(
+                out=wt_codes[:, a, cols].bitcast(FP8X4),
+                scales=wt_plane[:, a, cols],
+                in_=wt_bf[k][:].rearrange("p n i -> p (n i)"),
+            )
+
+        def move_t_scales(a):
+            for q in range(QUADS):
+                first = 16 * a + ROWS * q
+                nc.sync.dma_start(out=t_planes[32 * q : 32 * q + ROWS, a, :], in_=s2_got[first : first + ROWS, :])
+
+        nc.sync.dma_start(list2[:], offs2)
+        nc.sync.dma_start(list1[:], offs)
+        nc.sync.dma_start(out=s2_win[0:32, :], in_=tab2_scales.rearrange("a q t -> (a q) t").bitcast(I32))
+        load_wt(pieces[0])
+        nc.sync.dma_start(out=s1_win[0:16, :], in_=tab_scales[0].bitcast(I32))
+        load_wt(pieces[1])
+        nc.sync.dma_start(out=w2_win[:], in_=words(tab2_words))
+
+        nc.vector.memset(t_planes[:], 0)
+        nc.vector.memset(v_plane[:], 0)
+        for plane, scales in ((0, wv_scales), (1, zv_scales)):
+            for q in range(QUADS):
+                rows = scales[0, ROWS * q : ROWS * (q + 1), :]
+                nc.gpsimd.dma_start(out=w_planes[32 * q : 32 * q + ROWS, plane, :], in_=rows.bitcast(I32))
+        with nc.allow_non_contiguous_dma(reason="one bias value for each partition"):
+            nc.gpsimd.dma_start(out=b_sb[:], in_=b.rearrange("(c p) -> p c", p=P))
+        for q in range(QUADS):
+            rows = zt_scales[:, ROWS * q : ROWS * (q + 1), :].rearrange("a r n -> r a n")
+            nc.gpsimd.dma_start(out=w_planes[32 * q : 32 * q + ROWS, 2:4, :], in_=rows.bitcast(I32))
+
+        nc.vector.tensor_copy(out=s2_got[:].bitcast(U8), in_=s2_win[:].bitcast(U8).indirect(list2[:]))
+        cast(pieces[0])
+        cast(pieces[1])
+        move_t_scales(0)
+        nc.sync.dma_start(out=w1_win[:], in_=words(tab_words))
+        move_t_scales(1)
+        nc.sync.dma_start(out=wv_sb[:], in_=words(wv_words))
+        nc.sync.dma_start(out=zv_sb[:], in_=words(zv_words))
+        nc.sync.dma_start(out=zt_sb[:], in_=zt_words.rearrange("a p n -> p a n").bitcast(I32))
+        nc.vector.tensor_copy(out=s1_got[:].bitcast(U8), in_=s1_win[:].bitcast(U8).indirect(list1[:]))
+        for q in range(QUADS):
+            nc.sync.dma_start(out=v_plane[32 * q : 32 * q + ROWS, :], in_=s1_got[ROWS * q : ROWS * (q + 1), :])
+        load_wt(pieces[2])
+        load_wt(pieces[3])
+        quantise(pieces[0])
+        quantise(pieces[1])
+        nc.scalar.mul(half_b[:], b_sb[:], 0.5)
+
+        def entries(lst, c):
+            return lst[:, c * JC // 16 : (c + 1) * JC // 16]
+
+        def gather_t(c):
+            nc.vector.tensor_copy(out=t_got[c][:], in_=w2_win[:].bitcast(U32).indirect(entries(list2, c)))
+            nc.vector.tensor_copy(
+                out=t_part[c][:].bitcast(U16), in_=t_got[c][:].bitcast(U16).rearrange("p (j d) -> p d j", d=2)
+            )
+
+        def gather_v(c):
+            nc.vector.tensor_copy(out=v_got[c][:], in_=w1_win[:].bitcast(U32).indirect(entries(list1, c)))
+
+        def v_pass(acc, weights, plane, c, t, start, stop):
+            nc.tensor.matmul_mx(
+                out=acc[:],
+                lhsT=weights[:, M * t : M * (t + 1)].bitcast(FP8X4),
+                lhsT_scale=w_planes[:, plane, :].bitcast(U8)[:, M * t : M * (t + 1)],
+                rhs=v_got[c][:].bitcast(FP8X4),
+                rhs_scale=v_plane[:].bitcast(U8)[:, JC * c : JC * (c + 1)],
+                start=start,
+                stop=stop,
+            )
+
+        def t_pass(acc, lhsT, lhsT_scale, c, a, start, stop):
+            nc.tensor.matmul_mx(
+                out=acc[:],
+                lhsT=lhsT,
+                lhsT_scale=lhsT_scale,
+                rhs=t_part[c][:, a, :].bitcast(FP4X4),
+                rhs_scale=t_planes[:, a, :].bitcast(U8)[:, JC * c : JC * (c + 1)],
+                start=start,
+                stop=stop,
+            )
+
+        at, av, gt, diff, mixed = {}, {}, {}, {}, {}
+
+        def text_branch(c, t):
+            acc = psum.tile([P, JC], F32, name="ht", bufs=2)
+            cols = slice(M * t, M * (t + 1))
+            for a in range(2):
+                t_pass(acc, wt_codes[:, a, cols].bitcast(FP8X4), wt_plane[:, a, cols], c, a, a == 0, a == 1)
+            at[c, t] = held("at%d%d" % (c, t), [P, JC], F32)
+            nc.scalar.activation(out=at[c, t][:], in_=acc[:], func=TANH)
+
+        def picture_branch(c, t):
+            acc = psum.tile([P, JC], F32, name="hv", bufs=3)
+            v_pass(acc, wv_sb, 0, c, t, True, True)
+            av[c, t] = held("av%d%d" % (c, t), [P, JC], F32)
+            nc.scalar.activation(out=av[c, t][:], in_=acc[:], func=TANH)
+
+        def gate_branch(c, t):
+            acc = psum.tile([P, JC], F32, name="z", bufs=3)
+            v_pass(acc, zv_sb, 1, c, t, True, False)
+            for a in range(2):
+                codes = zt_sb[:, a, :].bitcast(U8)[:, 2 * M * t : 2 * M * (t + 1)].bitcast(FP4X4)
+                scale = w_planes[:, 2 + a, :].bitcast(U8)[:, M * t : M * (t + 1)]
+                t_pass(acc, codes, scale, c, a, False, a == 1)
+            gt[c, t] = held("gt%d%d" % (c, t), [P, JC], F32)
+            nc.scalar.activation(out=gt[c, t][:], in_=acc[:], func=TANH, bias=half_b[:, t : t + 1], scale=0.5)
+
+        def subtract(k):
+            diff[k] = work.tile([P, JC], F32, name="diff")
+            nc.vector.tensor_tensor(out=diff[k][:], in0=av[k][:], in1=at[k][:], op=ALU.subtract)
+
+        def weigh(k):
+            mixed[k] = work.tile([P, JC], F32, name="mixed")
+            nc.vector.scalar_tensor_tensor(
+                out=mixed[k][:], in0=gt[k][:], scalar=1.0, in1=diff[k][:], op0=ALU.add, op1=ALU.mult
+            )
+
+        def finish(k):
+            c, t = k
+            result = held("result%d%d" % k, [P, JC], F32)
+            nc.vector.scalar_tensor_tensor(
+                out=result[:], in0=mixed[k][:], scalar=0.5, in1=at[k][:], op0=ALU.mult, op1=ALU.add
+            )
+            nc.sync.dma_start(out=out[M * t : M * (t + 1), JC * c : JC * (c + 1)], in_=result[:])
+
+        gather_t(0)
+        gather_v(0)
+        gather_t(1)
+        gather_v(1)
+        blocks = [(c, 2 * h + u) for h in range(2) for c in range(J_CHUNKS) for u in range(2)]
+        for k in blocks[:4]:
+            text_branch(*k)
+        for s in range(len(blocks) + 2):
+            if s == 2:
+                for k in pieces[2:]:
+                    cast(k)
+                    quantise(k)
+            if s < len(blocks):
+                c, t = blocks[s]
+                if s >= 4:
+                    text_branch(c, t)
+                picture_branch(c, t)
+                gate_branch(c, t)
+                subtract(blocks[s])
+            if 2 <= s:
+                finish(blocks[s - 2])
+            if 1 <= s <= len(blocks):
+                weigh(blocks[s - 1])

@@ -40,13 +40,14 @@ def tile_list_gmu_tanh_none_kernel(
         def held(name, shape, dtype):
             return keep.tile(shape, dtype, name=name, align_bytes=64)
 
+        def shared(name, tag, shape, dtype):
+            return keep.tile(shape, dtype, name=name, tag=tag, align_bytes=64)
+
         list1 = keep.tile([P, J // 16], U16, name="list1")
         list2 = keep.tile([P, J // 16], U16, name="list2")
         s1_win = held("s1_win", [P, T // 4], I32)
-        s2_win = held("s2_win", [P, T // 4], I32)
-        s1_got = held("s1_got", [P, J // 4], I32)
+        s2_win = shared("s2_win", "early", [P, T // 4], I32)
         s2_got = held("s2_got", [P, J // 4], I32)
-        v_plane = held("v_plane", [P, J // 4], I32)
         t_planes = held("t_planes", [P, 2, J // 4], I32)
         w_planes = held("w_planes", [P, 4, N // 4], I32)
         w1_win = held("w1_win", [P, T], I32)
@@ -54,7 +55,6 @@ def tile_list_gmu_tanh_none_kernel(
         zv_sb = held("zv_sb", [P, N], I32)
         zt_sb = held("zt_sb", [P, 2, N // 2], I32)
         w2_win = held("w2_win", [P, T], I32)
-        b_sb = held("b_sb", [P, N_TILES], F32)
         half_b = held("half_b", [P, N_TILES], F32)
         wt_codes = held("wt_codes", [P, 2, N], U32)
         wt_plane = held("wt_plane", [P, 2, N], U8)
@@ -64,9 +64,11 @@ def tile_list_gmu_tanh_none_kernel(
         t_got = [held("t_got%d" % c, [P, JC], U32) for c in range(J_CHUNKS)]
         t_part = [held("t_part%d" % c, [P, 2, 2 * JC], U8) for c in range(J_CHUNKS)]
 
-        nc.vector.memset(s2_win[:], 0)
-        nc.vector.memset(s1_win[:], 0)
+        nc.vector.memset(s2_win[32:64, :], 0)
+        nc.vector.memset(s2_win[64:128, :], 0)
+        nc.gpsimd.memset(s1_win[:], 0)
         nc.gpsimd.memset(w_planes[:], 0)
+        nc.vector.memset(t_planes[:], 0)
 
         def load_wt(k):
             a, h = k
@@ -78,7 +80,7 @@ def tile_list_gmu_tanh_none_kernel(
             return ap[0].rearrange("p n i -> p (n i)").bitcast(I32)
 
         def cast(k):
-            wt_bf[k] = held("wt_bf%d%d" % k, [P, NH, PACK], BF16)
+            wt_bf[k] = shared("wt_bf%d%d" % k, "bf%d%d" % k, [P, NH, PACK], BF16)
             nc.scalar.copy(
                 out=wt_bf[k][:].rearrange("p (c n) i -> p c i n", n=4),
                 in_=wt_raw[k][:].rearrange("p i (c n) -> p c i n", n=4),
@@ -98,43 +100,39 @@ def tile_list_gmu_tanh_none_kernel(
                 first = 16 * a + ROWS * q
                 nc.sync.dma_start(out=t_planes[32 * q : 32 * q + ROWS, a, :], in_=s2_got[first : first + ROWS, :])
 
-        nc.sync.dma_start(list2[:], offs2)
-        nc.sync.dma_start(list1[:], offs)
-        nc.sync.dma_start(out=s2_win[0:32, :], in_=tab2_scales.rearrange("a q t -> (a q) t").bitcast(I32))
-        load_wt(pieces[0])
-        nc.sync.dma_start(out=s1_win[0:16, :], in_=tab_scales[0].bitcast(I32))
-        load_wt(pieces[1])
-        nc.sync.dma_start(out=w2_win[:], in_=words(tab2_words))
-
-        nc.vector.memset(t_planes[:], 0)
-        nc.vector.memset(v_plane[:], 0)
-        for plane, scales in ((0, wv_scales), (1, zv_scales)):
+        def load_plane(queue, plane, scales):
             for q in range(QUADS):
                 rows = scales[0, ROWS * q : ROWS * (q + 1), :]
-                nc.gpsimd.dma_start(out=w_planes[32 * q : 32 * q + ROWS, plane, :], in_=rows.bitcast(I32))
-        with nc.allow_non_contiguous_dma(reason="one bias value for each partition"):
-            nc.gpsimd.dma_start(out=b_sb[:], in_=b.rearrange("(c p) -> p c", p=P))
+                queue.dma_start(out=plane[32 * q : 32 * q + ROWS, :], in_=rows.bitcast(I32))
+
+        nc.sync.dma_start(list2[:], offs2)
+        nc.sync.dma_start(out=s2_win[0:32, :], in_=tab2_scales.rearrange("a q t -> (a q) t").bitcast(I32))
+        nc.sync.dma_start(out=w2_win[:], in_=words(tab2_words))
+        nc.sync.dma_start(list1[:], offs)
+        load_plane(nc.sync, s1_win, tab_scales)
+        load_wt(pieces[0])
+        load_wt(pieces[1])
         for q in range(QUADS):
             rows = zt_scales[:, ROWS * q : ROWS * (q + 1), :].rearrange("a r n -> r a n")
             nc.gpsimd.dma_start(out=w_planes[32 * q : 32 * q + ROWS, 2:4, :], in_=rows.bitcast(I32))
 
         nc.vector.tensor_copy(out=s2_got[:].bitcast(U8), in_=s2_win[:].bitcast(U8).indirect(list2[:]))
-        cast(pieces[0])
-        cast(pieces[1])
         move_t_scales(0)
-        nc.sync.dma_start(out=w1_win[:], in_=words(tab_words))
+        load_wt(pieces[2])
+        load_wt(pieces[3])
         move_t_scales(1)
+        nc.sync.dma_start(out=w1_win[:], in_=words(tab_words))
+        load_plane(nc.sync, w_planes[:, 0, :], wv_scales)
         nc.sync.dma_start(out=wv_sb[:], in_=words(wv_words))
         nc.sync.dma_start(out=zv_sb[:], in_=words(zv_words))
         nc.sync.dma_start(out=zt_sb[:], in_=zt_words.rearrange("a p n -> p a n").bitcast(I32))
-        nc.vector.tensor_copy(out=s1_got[:].bitcast(U8), in_=s1_win[:].bitcast(U8).indirect(list1[:]))
-        for q in range(QUADS):
-            nc.sync.dma_start(out=v_plane[32 * q : 32 * q + ROWS, :], in_=s1_got[ROWS * q : ROWS * (q + 1), :])
-        load_wt(pieces[2])
-        load_wt(pieces[3])
-        quantise(pieces[0])
-        quantise(pieces[1])
-        nc.scalar.mul(half_b[:], b_sb[:], 0.5)
+        load_plane(nc.sync, w_planes[:, 1, :], zv_scales)
+        b_sb = shared("b_sb", "early", [P, N_TILES], F32)
+        with nc.allow_non_contiguous_dma(reason="one bias value for each partition"):
+            nc.gpsimd.dma_start(out=b_sb[:], in_=b.rearrange("(c p) -> p c", p=P))
+        nc.gpsimd.tensor_scalar(
+            out=half_b[:], in0=b_sb[:], scalar1=0.5, scalar2=0.0, op0=ALU.mult, op1=ALU.add
+        )
 
         def entries(lst, c):
             return lst[:, c * JC // 16 : (c + 1) * JC // 16]
@@ -154,7 +152,7 @@ def tile_list_gmu_tanh_none_kernel(
                 lhsT=weights[:, M * t : M * (t + 1)].bitcast(FP8X4),
                 lhsT_scale=w_planes[:, plane, :].bitcast(U8)[:, M * t : M * (t + 1)],
                 rhs=v_got[c][:].bitcast(FP8X4),
-                rhs_scale=v_plane[:].bitcast(U8)[:, JC * c : JC * (c + 1)],
+                rhs_scale=v_plane[:, JC * c : JC * (c + 1)],
                 start=start,
                 stop=stop,
             )
@@ -172,8 +170,8 @@ def tile_list_gmu_tanh_none_kernel(
 
         at, av, gt, diff, mixed = {}, {}, {}, {}, {}
 
-        def text_branch(c, t):
-            acc = psum.tile([P, JC], F32, name="ht", bufs=2)
+        def text_branch(c, t, tag, bufs):
+            acc = psum.tile([P, JC], F32, name="ht", tag=tag, bufs=bufs)
             cols = slice(M * t, M * (t + 1))
             for a in range(2):
                 t_pass(acc, wt_codes[:, a, cols].bitcast(FP8X4), wt_plane[:, a, cols], c, a, a == 0, a == 1)
@@ -181,13 +179,13 @@ def tile_list_gmu_tanh_none_kernel(
             nc.scalar.activation(out=at[c, t][:], in_=acc[:], func=TANH)
 
         def picture_branch(c, t):
-            acc = psum.tile([P, JC], F32, name="hv", bufs=3)
+            acc = psum.tile([P, JC], F32, name="hv", tag="late", bufs=6)
             v_pass(acc, wv_sb, 0, c, t, True, True)
             av[c, t] = held("av%d%d" % (c, t), [P, JC], F32)
             nc.scalar.activation(out=av[c, t][:], in_=acc[:], func=TANH)
 
         def gate_branch(c, t):
-            acc = psum.tile([P, JC], F32, name="z", bufs=3)
+            acc = psum.tile([P, JC], F32, name="z", tag="late", bufs=6)
             v_pass(acc, zv_sb, 1, c, t, True, False)
             for a in range(2):
                 codes = zt_sb[:, a, :].bitcast(U8)[:, 2 * M * t : 2 * M * (t + 1)].bitcast(FP4X4)
@@ -215,23 +213,26 @@ def tile_list_gmu_tanh_none_kernel(
             nc.sync.dma_start(out=out[M * t : M * (t + 1), JC * c : JC * (c + 1)], in_=result[:])
 
         gather_t(0)
-        gather_v(0)
+        for k in pieces[:2]:
+            cast(k)
+            quantise(k)
         gather_t(1)
+        v_plane = shared("v_plane", "bf%d%d" % pieces[1], [P, J], U8)
+        nc.vector.tensor_copy(out=v_plane[:], in_=s1_win[:].bitcast(U8).indirect(list1[:]))
+        for k in pieces[2:]:
+            cast(k)
+            quantise(k)
+        gather_v(0)
         gather_v(1)
-        blocks = [(c, 2 * h + u) for h in range(2) for c in range(J_CHUNKS) for u in range(2)]
-        for k in blocks[:4]:
-            text_branch(*k)
+        blocks = [(c, t) for c in range(J_CHUNKS) for t in range(N_TILES)]
+        for k in [(0, 0), (0, 1), (1, 0), (0, 2), (0, 3)]:
+            text_branch(*k, "early", 2)
         for s in range(len(blocks) + 2):
-            if s == 2:
-                for k in pieces[2:]:
-                    cast(k)
-                    quantise(k)
             if s < len(blocks):
-                c, t = blocks[s]
-                if s >= 4:
-                    text_branch(c, t)
-                picture_branch(c, t)
-                gate_branch(c, t)
+                picture_branch(*blocks[s])
+                gate_branch(*blocks[s])
+                if 2 <= s <= 4:
+                    text_branch(*blocks[s + 3], "late", 6)
                 subtract(blocks[s])
             if 2 <= s:
                 finish(blocks[s - 2])

@@ -25,6 +25,8 @@ N_TILES = N // M
 JC = 512
 J_CHUNKS = J // JC
 NH = 256
+V_SHIFT = 4
+W_SHIFT = 8
 
 
 def tile_list_gmu_tanh_none_kernel(
@@ -100,21 +102,22 @@ def tile_list_gmu_tanh_none_kernel(
                 first = 16 * a + ROWS * q
                 nc.sync.dma_start(out=t_planes[32 * q : 32 * q + ROWS, a, :], in_=s2_got[first : first + ROWS, :])
 
-        def load_plane(queue, plane, scales):
+        def load_plane(queue, plane, scales, shift):
             for q in range(QUADS):
                 rows = scales[0, ROWS * q : ROWS * (q + 1), :]
-                queue.dma_start(out=plane[32 * q : 32 * q + ROWS, :], in_=rows.bitcast(I32))
+                queue.dma_start(out=plane[32 * q + shift : 32 * q + shift + ROWS, :], in_=rows.bitcast(I32))
 
         nc.sync.dma_start(list2[:], offs2)
         nc.sync.dma_start(out=s2_win[0:32, :], in_=tab2_scales.rearrange("a q t -> (a q) t").bitcast(I32))
         nc.sync.dma_start(out=w2_win[:], in_=words(tab2_words))
         nc.sync.dma_start(list1[:], offs)
-        load_plane(nc.sync, s1_win, tab_scales)
+        load_plane(nc.sync, s1_win, tab_scales, V_SHIFT)
         load_wt(pieces[0])
         load_wt(pieces[1])
         for q in range(QUADS):
             rows = zt_scales[:, ROWS * q : ROWS * (q + 1), :].rearrange("a r n -> r a n")
             nc.gpsimd.dma_start(out=w_planes[32 * q : 32 * q + ROWS, 2:4, :], in_=rows.bitcast(I32))
+        load_plane(nc.gpsimd, w_planes[:, 1, :], zv_scales, W_SHIFT)
 
         nc.vector.tensor_copy(out=s2_got[:].bitcast(U8), in_=s2_win[:].bitcast(U8).indirect(list2[:]))
         move_t_scales(0)
@@ -122,11 +125,10 @@ def tile_list_gmu_tanh_none_kernel(
         load_wt(pieces[3])
         move_t_scales(1)
         nc.sync.dma_start(out=w1_win[:], in_=words(tab_words))
-        load_plane(nc.sync, w_planes[:, 0, :], wv_scales)
+        load_plane(nc.sync, w_planes[:, 0, :], wv_scales, W_SHIFT)
         nc.sync.dma_start(out=wv_sb[:], in_=words(wv_words))
         nc.sync.dma_start(out=zv_sb[:], in_=words(zv_words))
         nc.sync.dma_start(out=zt_sb[:], in_=zt_words.rearrange("a p n -> p a n").bitcast(I32))
-        load_plane(nc.sync, w_planes[:, 1, :], zv_scales)
         b_sb = shared("b_sb", "early", [P, N_TILES], F32)
         with nc.allow_non_contiguous_dma(reason="one bias value for each partition"):
             nc.gpsimd.dma_start(out=b_sb[:], in_=b.rearrange("(c p) -> p c", p=P))
@@ -150,9 +152,9 @@ def tile_list_gmu_tanh_none_kernel(
             nc.tensor.matmul_mx(
                 out=acc[:],
                 lhsT=weights[:, M * t : M * (t + 1)].bitcast(FP8X4),
-                lhsT_scale=w_planes[:, plane, :].bitcast(U8)[:, M * t : M * (t + 1)],
+                lhsT_scale=w_planes[W_SHIFT:, plane, :].bitcast(U8)[:, M * t : M * (t + 1)],
                 rhs=v_got[c][:].bitcast(FP8X4),
-                rhs_scale=v_plane[:, JC * c : JC * (c + 1)],
+                rhs_scale=v_plane[V_SHIFT:, JC * c : JC * (c + 1)],
                 start=start,
                 stop=stop,
             )
@@ -179,13 +181,13 @@ def tile_list_gmu_tanh_none_kernel(
             nc.scalar.activation(out=at[c, t][:], in_=acc[:], func=TANH)
 
         def picture_branch(c, t):
-            acc = psum.tile([P, JC], F32, name="hv", tag="late", bufs=6)
+            acc = psum.tile([P, JC], F32, name="hv", tag="late", bufs=5)
             v_pass(acc, wv_sb, 0, c, t, True, True)
             av[c, t] = held("av%d%d" % (c, t), [P, JC], F32)
             nc.scalar.activation(out=av[c, t][:], in_=acc[:], func=TANH)
 
         def gate_branch(c, t):
-            acc = psum.tile([P, JC], F32, name="z", tag="late", bufs=6)
+            acc = psum.tile([P, JC], F32, name="z", tag="late", bufs=5)
             v_pass(acc, zv_sb, 1, c, t, True, False)
             for a in range(2):
                 codes = zt_sb[:, a, :].bitcast(U8)[:, 2 * M * t : 2 * M * (t + 1)].bitcast(FP4X4)
@@ -204,13 +206,16 @@ def tile_list_gmu_tanh_none_kernel(
                 out=mixed[k][:], in0=gt[k][:], scalar=1.0, in1=diff[k][:], op0=ALU.add, op1=ALU.mult
             )
 
-        def finish(k):
+        def finish(k, parts):
             c, t = k
             result = held("result%d%d" % k, [P, JC], F32)
-            nc.vector.scalar_tensor_tensor(
-                out=result[:], in0=mixed[k][:], scalar=0.5, in1=at[k][:], op0=ALU.mult, op1=ALU.add
-            )
-            nc.sync.dma_start(out=out[M * t : M * (t + 1), JC * c : JC * (c + 1)], in_=result[:])
+            for first, last in parts:
+                cols = slice(first, last)
+                nc.vector.scalar_tensor_tensor(
+                    out=result[:, cols], in0=mixed[k][:, cols], scalar=0.5, in1=at[k][:, cols],
+                    op0=ALU.mult, op1=ALU.add,
+                )
+                nc.sync.dma_start(out=out[M * t : M * (t + 1), JC * c + first : JC * c + last], in_=result[:, cols])
 
         gather_t(0)
         for k in pieces[:2]:
@@ -226,15 +231,15 @@ def tile_list_gmu_tanh_none_kernel(
         gather_v(1)
         blocks = [(c, t) for c in range(J_CHUNKS) for t in range(N_TILES)]
         for k in [(0, 0), (0, 1), (1, 0), (0, 2), (0, 3)]:
-            text_branch(*k, "early", 2)
+            text_branch(*k, "early", 3)
         for s in range(len(blocks) + 2):
             if s < len(blocks):
+                if s > 4:
+                    text_branch(*blocks[s], "late", 5)
                 picture_branch(*blocks[s])
                 gate_branch(*blocks[s])
-                if 2 <= s <= 4:
-                    text_branch(*blocks[s + 3], "late", 6)
                 subtract(blocks[s])
             if 2 <= s:
-                finish(blocks[s - 2])
+                finish(blocks[s - 2], [(0, JC)])
             if 1 <= s <= len(blocks):
                 weigh(blocks[s - 1])

@@ -26,7 +26,6 @@ JC = 512
 J_CHUNKS = J // JC
 NH = 256
 V_SHIFT = 4
-W_SHIFT = 8
 
 
 def tile_list_gmu_tanh_none_kernel(
@@ -53,9 +52,9 @@ def tile_list_gmu_tanh_none_kernel(
         t_planes = held("t_planes", [P, 2, J // 4], I32)
         w_planes = held("w_planes", [P, 4, N // 4], I32)
         w1_win = held("w1_win", [P, T], I32)
-        wv_sb = held("wv_sb", [P, N], I32)
-        zv_sb = held("zv_sb", [P, N], I32)
-        zt_sb = held("zt_sb", [P, 2, N // 2], I32)
+        wv_sb = [held("wv_sb%d" % h, [P, NH], I32) for h in range(N // NH)]
+        zv_sb = [held("zv_sb%d" % h, [P, NH], I32) for h in range(N // NH)]
+        zt_sb = [held("zt_sb%d" % h, [P, 2, NH // 2], I32) for h in range(N // NH)]
         w2_win = held("w2_win", [P, T], I32)
         half_b = held("half_b", [P, N_TILES], F32)
         wt_codes = held("wt_codes", [P, 2, N], U32)
@@ -66,15 +65,15 @@ def tile_list_gmu_tanh_none_kernel(
         t_got = [held("t_got%d" % c, [P, JC], U32) for c in range(J_CHUNKS)]
         t_part = [held("t_part%d" % c, [P, 2, 2 * JC], U8) for c in range(J_CHUNKS)]
 
-        nc.vector.memset(s2_win[32:64, :], 0)
-        nc.vector.memset(s2_win[64:128, :], 0)
         nc.gpsimd.memset(s1_win[:], 0)
         nc.gpsimd.memset(w_planes[:], 0)
-        nc.vector.memset(t_planes[:], 0)
+        nc.vector.memset(s2_win[32:64, :], 0)
+        nc.vector.memset(s2_win[64:128, :], 0)
+        nc.gpsimd.memset(t_planes[:], 0)
 
         def load_wt(k):
             a, h = k
-            wt_raw[k] = held("wt_raw%d%d" % k, [P, PACK, NH], F32)
+            wt_raw[k] = shared("wt_raw%d%d" % k, "raw%d%d" % k, [P, PACK, NH], F32)
             rows = wt[512 * a : 512 * (a + 1), NH * h : NH * (h + 1)]
             nc.sync.dma_start(out=wt_raw[k][:], in_=rows.rearrange("(p i) n -> p i n", i=PACK))
 
@@ -82,7 +81,7 @@ def tile_list_gmu_tanh_none_kernel(
             return ap[0].rearrange("p n i -> p (n i)").bitcast(I32)
 
         def cast(k):
-            wt_bf[k] = shared("wt_bf%d%d" % k, "bf%d%d" % k, [P, NH, PACK], BF16)
+            wt_bf[k] = held("wt_bf%d%d" % k, [P, NH, PACK], BF16)
             nc.scalar.copy(
                 out=wt_bf[k][:].rearrange("p (c n) i -> p c i n", n=4),
                 in_=wt_raw[k][:].rearrange("p i (c n) -> p c i n", n=4),
@@ -97,50 +96,60 @@ def tile_list_gmu_tanh_none_kernel(
                 in_=wt_bf[k][:].rearrange("p n i -> p (n i)"),
             )
 
-        def move_t_scales(a):
+        def move_t_scales():
             for q in range(QUADS):
-                first = 16 * a + ROWS * q
-                nc.sync.dma_start(out=t_planes[32 * q : 32 * q + ROWS, a, :], in_=s2_got[first : first + ROWS, :])
+                rows = s2_got[2 * ROWS * q : 2 * ROWS * (q + 1), :]
+                nc.sync.dma_start(out=t_planes[32 * q : 32 * q + ROWS, :, :], in_=rows)
 
         def load_plane(queue, plane, scales, shift):
-            for q in range(QUADS):
-                rows = scales[0, ROWS * q : ROWS * (q + 1), :]
-                queue.dma_start(out=plane[32 * q + shift : 32 * q + shift + ROWS, :], in_=rows.bitcast(I32))
+            for r in range(ROWS):
+                rows = scales[0, r::ROWS, :]
+                queue.dma_start(out=plane[shift + r : P : 32, :], in_=rows.bitcast(I32))
+
+        def load_weight_scales(queue, first, scales):
+            passes = scales.shape[0]
+            rows = scales.rearrange("a q n -> q a n").bitcast(I32)
+            queue.dma_start(out=w_planes[0 : QUADS * ROWS, first : first + passes, :], in_=rows)
 
         nc.sync.dma_start(list2[:], offs2)
-        nc.sync.dma_start(out=s2_win[0:32, :], in_=tab2_scales.rearrange("a q t -> (a q) t").bitcast(I32))
-        nc.sync.dma_start(out=w2_win[:], in_=words(tab2_words))
+        nc.sync.dma_start(out=s2_win[0:32, :], in_=tab2_scales.rearrange("a q t -> q a t").bitcast(I32))
         nc.sync.dma_start(list1[:], offs)
+        nc.sync.dma_start(out=w2_win[:], in_=words(tab2_words))
         load_plane(nc.sync, s1_win, tab_scales, V_SHIFT)
-        load_wt(pieces[0])
-        load_wt(pieces[1])
-        for q in range(QUADS):
-            rows = zt_scales[:, ROWS * q : ROWS * (q + 1), :].rearrange("a r n -> r a n")
-            nc.gpsimd.dma_start(out=w_planes[32 * q : 32 * q + ROWS, 2:4, :], in_=rows.bitcast(I32))
-        load_plane(nc.gpsimd, w_planes[:, 1, :], zv_scales, W_SHIFT)
+        load_weight_scales(nc.sync, 2, zt_scales)
+        load_weight_scales(nc.gpsimd, 1, zv_scales)
+        for k in pieces[:3]:
+            load_wt(k)
 
         nc.vector.tensor_copy(out=s2_got[:].bitcast(U8), in_=s2_win[:].bitcast(U8).indirect(list2[:]))
-        move_t_scales(0)
-        load_wt(pieces[2])
-        load_wt(pieces[3])
-        move_t_scales(1)
-        nc.sync.dma_start(out=w1_win[:], in_=words(tab_words))
-        load_plane(nc.sync, w_planes[:, 0, :], wv_scales, W_SHIFT)
-        nc.sync.dma_start(out=wv_sb[:], in_=words(wv_words))
-        nc.sync.dma_start(out=zv_sb[:], in_=words(zv_words))
-        nc.sync.dma_start(out=zt_sb[:], in_=zt_words.rearrange("a p n -> p a n").bitcast(I32))
+        move_t_scales()
         b_sb = shared("b_sb", "early", [P, N_TILES], F32)
         with nc.allow_non_contiguous_dma(reason="one bias value for each partition"):
             nc.gpsimd.dma_start(out=b_sb[:], in_=b.rearrange("(c p) -> p c", p=P))
         nc.gpsimd.tensor_scalar(
             out=half_b[:], in0=b_sb[:], scalar1=0.5, scalar2=0.0, op0=ALU.mult, op1=ALU.add
         )
+        load_weight_scales(nc.sync, 0, wv_scales)
+        nc.sync.dma_start(out=w1_win[:], in_=words(tab_words))
+        for q in range(1, QUADS):
+            nc.sync.dma_start(
+                out=w_planes[32 * q : 32 * q + ROWS, :, :], in_=w_planes[ROWS * q : ROWS * (q + 1), :, :]
+            )
+        for h in range(N // NH):
+            cols = slice(NH * h, NH * (h + 1))
+            halves = slice(NH // 2 * h, NH // 2 * (h + 1))
+            nc.sync.dma_start(out=wv_sb[h][:], in_=words(wv_words)[:, cols])
+            nc.sync.dma_start(out=zt_sb[h][:], in_=zt_words.rearrange("a p n -> p a n").bitcast(I32)[:, :, halves])
+            nc.sync.dma_start(out=zv_sb[h][:], in_=words(zv_words)[:, cols])
+        load_wt(pieces[3])
 
         def entries(lst, c):
             return lst[:, c * JC // 16 : (c + 1) * JC // 16]
 
         def gather_t(c):
             nc.vector.tensor_copy(out=t_got[c][:], in_=w2_win[:].bitcast(U32).indirect(entries(list2, c)))
+
+        def part_t(c):
             nc.vector.tensor_copy(
                 out=t_part[c][:].bitcast(U16), in_=t_got[c][:].bitcast(U16).rearrange("p (j d) -> p d j", d=2)
             )
@@ -151,8 +160,8 @@ def tile_list_gmu_tanh_none_kernel(
         def v_pass(acc, weights, plane, c, t, start, stop):
             nc.tensor.matmul_mx(
                 out=acc[:],
-                lhsT=weights[:, M * t : M * (t + 1)].bitcast(FP8X4),
-                lhsT_scale=w_planes[W_SHIFT:, plane, :].bitcast(U8)[:, M * t : M * (t + 1)],
+                lhsT=weights[t // 2][:, M * (t % 2) : M * (t % 2 + 1)].bitcast(FP8X4),
+                lhsT_scale=w_planes[:, plane, :].bitcast(U8)[:, M * t : M * (t + 1)],
                 rhs=v_got[c][:].bitcast(FP8X4),
                 rhs_scale=v_plane[V_SHIFT:, JC * c : JC * (c + 1)],
                 start=start,
@@ -190,7 +199,7 @@ def tile_list_gmu_tanh_none_kernel(
             acc = psum.tile([P, JC], F32, name="z", tag="late", bufs=5)
             v_pass(acc, zv_sb, 1, c, t, True, False)
             for a in range(2):
-                codes = zt_sb[:, a, :].bitcast(U8)[:, 2 * M * t : 2 * M * (t + 1)].bitcast(FP4X4)
+                codes = zt_sb[t // 2][:, a, :].bitcast(U8)[:, 2 * M * (t % 2) : 2 * M * (t % 2 + 1)].bitcast(FP4X4)
                 scale = w_planes[:, 2 + a, :].bitcast(U8)[:, M * t : M * (t + 1)]
                 t_pass(acc, codes, scale, c, a, False, a == 1)
             gt[c, t] = held("gt%d%d" % (c, t), [P, JC], F32)
@@ -200,11 +209,14 @@ def tile_list_gmu_tanh_none_kernel(
             diff[k] = work.tile([P, JC], F32, name="diff")
             nc.vector.tensor_tensor(out=diff[k][:], in0=av[k][:], in1=at[k][:], op=ALU.subtract)
 
-        def weigh(k):
+        def weigh(k, parts):
             mixed[k] = work.tile([P, JC], F32, name="mixed")
-            nc.vector.scalar_tensor_tensor(
-                out=mixed[k][:], in0=gt[k][:], scalar=1.0, in1=diff[k][:], op0=ALU.add, op1=ALU.mult
-            )
+            for first, last in parts:
+                cols = slice(first, last)
+                nc.vector.scalar_tensor_tensor(
+                    out=mixed[k][:, cols], in0=gt[k][:, cols], scalar=1.0, in1=diff[k][:, cols],
+                    op0=ALU.add, op1=ALU.mult,
+                )
 
         def finish(k, parts):
             c, t = k
@@ -217,29 +229,37 @@ def tile_list_gmu_tanh_none_kernel(
                 )
                 nc.sync.dma_start(out=out[M * t : M * (t + 1), JC * c + first : JC * c + last], in_=result[:, cols])
 
-        gather_t(0)
+        for c in range(J_CHUNKS):
+            gather_t(c)
+        for c in range(J_CHUNKS):
+            part_t(c)
         for k in pieces[:2]:
             cast(k)
             quantise(k)
-        gather_t(1)
-        v_plane = shared("v_plane", "bf%d%d" % pieces[1], [P, J], U8)
+        v_plane = shared("v_plane", "raw%d%d" % pieces[1], [P, J], U8)
         nc.vector.tensor_copy(out=v_plane[:], in_=s1_win[:].bitcast(U8).indirect(list1[:]))
-        for k in pieces[2:]:
-            cast(k)
-            quantise(k)
+        cast(pieces[2])
+        quantise(pieces[2])
         gather_v(0)
         gather_v(1)
-        blocks = [(c, t) for c in range(J_CHUNKS) for t in range(N_TILES)]
-        for k in [(0, 0), (0, 1), (1, 0), (0, 2), (0, 3)]:
+        blocks = [(c, 2 * h + t) for h in range(2) for c in range(J_CHUNKS) for t in range(2)]
+
+        def parts(s):
+            return [(0, JC // 2), (JC // 2, JC)] if s == len(blocks) - 1 else [(0, JC)]
+
+        for k in blocks[:3]:
             text_branch(*k, "early", 3)
         for s in range(len(blocks) + 2):
             if s < len(blocks):
-                if s > 4:
+                if s == 2:
+                    cast(pieces[3])
+                    quantise(pieces[3])
+                if s >= 3:
                     text_branch(*blocks[s], "late", 5)
                 picture_branch(*blocks[s])
                 gate_branch(*blocks[s])
                 subtract(blocks[s])
             if 2 <= s:
-                finish(blocks[s - 2], [(0, JC)])
+                finish(blocks[s - 2], parts(s - 2))
             if 1 <= s <= len(blocks):
-                weigh(blocks[s - 1])
+                weigh(blocks[s - 1], parts(s - 1))

@@ -26,6 +26,7 @@ JC = 512
 J_CHUNKS = J // JC
 NH = 256
 V_SHIFT = 4
+EARLY = 4
 
 
 def tile_list_gmu_tanh_none_kernel(
@@ -63,7 +64,7 @@ def tile_list_gmu_tanh_none_kernel(
         wt_raw, wt_bf = {}, {}
         v_got = [held("v_got%d" % c, [P, JC], U32) for c in range(J_CHUNKS)]
         t_got = [held("t_got%d" % c, [P, JC], U32) for c in range(J_CHUNKS)]
-        t_part = [held("t_part%d" % c, [P, 2, 2 * JC], U8) for c in range(J_CHUNKS)]
+        t_part = {}
 
         nc.gpsimd.memset(s1_win[:], 0)
         nc.gpsimd.memset(w_planes[:], 0)
@@ -118,11 +119,12 @@ def tile_list_gmu_tanh_none_kernel(
         load_plane(nc.sync, s1_win, tab_scales, V_SHIFT)
         load_weight_scales(nc.sync, 2, zt_scales)
         load_weight_scales(nc.gpsimd, 1, zv_scales)
-        for k in pieces[:3]:
+        for k in pieces[:2]:
             load_wt(k)
 
         nc.vector.tensor_copy(out=s2_got[:].bitcast(U8), in_=s2_win[:].bitcast(U8).indirect(list2[:]))
         move_t_scales()
+        load_wt(pieces[2])
         b_sb = shared("b_sb", "early", [P, N_TILES], F32)
         with nc.allow_non_contiguous_dma(reason="one bias value for each partition"):
             nc.gpsimd.dma_start(out=b_sb[:], in_=b.rearrange("(c p) -> p c", p=P))
@@ -149,7 +151,8 @@ def tile_list_gmu_tanh_none_kernel(
         def gather_t(c):
             nc.vector.tensor_copy(out=t_got[c][:], in_=w2_win[:].bitcast(U32).indirect(entries(list2, c)))
 
-        def part_t(c):
+        def part_t(c, tag):
+            t_part[c] = shared("t_part%d" % c, tag, [P, 2, 2 * JC], U8)
             nc.vector.tensor_copy(
                 out=t_part[c][:].bitcast(U16), in_=t_got[c][:].bitcast(U16).rearrange("p (j d) -> p d j", d=2)
             )
@@ -186,17 +189,18 @@ def tile_list_gmu_tanh_none_kernel(
             cols = slice(M * t, M * (t + 1))
             for a in range(2):
                 t_pass(acc, wt_codes[:, a, cols].bitcast(FP8X4), wt_plane[:, a, cols], c, a, a == 0, a == 1)
-            at[c, t] = held("at%d%d" % (c, t), [P, JC], F32)
-            nc.scalar.activation(out=at[c, t][:], in_=acc[:], func=TANH)
+            if (c, t) not in at:
+                at[c, t] = held("at%d%d" % (c, t), [P, JC], F32)[:]
+            nc.scalar.activation(out=at[c, t], in_=acc[:], func=TANH)
 
         def picture_branch(c, t):
-            acc = psum.tile([P, JC], F32, name="hv", tag="late", bufs=5)
+            acc = psum.tile([P, JC], F32, name="hv", tag="late", bufs=8 - EARLY)
             v_pass(acc, wv_sb, 0, c, t, True, True)
             av[c, t] = held("av%d%d" % (c, t), [P, JC], F32)
             nc.scalar.activation(out=av[c, t][:], in_=acc[:], func=TANH)
 
         def gate_branch(c, t):
-            acc = psum.tile([P, JC], F32, name="z", tag="late", bufs=5)
+            acc = psum.tile([P, JC], F32, name="z", tag="late", bufs=8 - EARLY)
             v_pass(acc, zv_sb, 1, c, t, True, False)
             for a in range(2):
                 codes = zt_sb[t // 2][:, a, :].bitcast(U8)[:, 2 * M * (t % 2) : 2 * M * (t % 2 + 1)].bitcast(FP4X4)
@@ -207,7 +211,7 @@ def tile_list_gmu_tanh_none_kernel(
 
         def subtract(k):
             diff[k] = work.tile([P, JC], F32, name="diff")
-            nc.vector.tensor_tensor(out=diff[k][:], in0=av[k][:], in1=at[k][:], op=ALU.subtract)
+            nc.vector.tensor_tensor(out=diff[k][:], in0=av[k][:], in1=at[k], op=ALU.subtract)
 
         def weigh(k, parts):
             mixed[k] = work.tile([P, JC], F32, name="mixed")
@@ -231,11 +235,12 @@ def tile_list_gmu_tanh_none_kernel(
 
         for c in range(J_CHUNKS):
             gather_t(c)
-        for c in range(J_CHUNKS):
-            part_t(c)
-        for k in pieces[:2]:
-            cast(k)
-            quantise(k)
+        part_t(0, "t_part0")
+        cast(pieces[0])
+        quantise(pieces[0])
+        part_t(1, "raw%d%d" % pieces[0])
+        cast(pieces[1])
+        quantise(pieces[1])
         v_plane = shared("v_plane", "raw%d%d" % pieces[1], [P, J], U8)
         nc.vector.tensor_copy(out=v_plane[:], in_=s1_win[:].bitcast(U8).indirect(list1[:]))
         cast(pieces[2])
@@ -247,15 +252,17 @@ def tile_list_gmu_tanh_none_kernel(
         def parts(s):
             return [(0, JC // 2), (JC // 2, JC)] if s == len(blocks) - 1 else [(0, JC)]
 
-        for k in blocks[:3]:
-            text_branch(*k, "early", 3)
+        at_early = shared("at_early", "raw%d%d" % pieces[2], [P, EARLY, JC], F32)
+        for s, k in enumerate(blocks[:EARLY]):
+            at[k] = at_early[:, s, :]
+            text_branch(*k, "early", EARLY)
         for s in range(len(blocks) + 2):
             if s < len(blocks):
                 if s == 2:
                     cast(pieces[3])
                     quantise(pieces[3])
-                if s >= 3:
-                    text_branch(*blocks[s], "late", 5)
+                if s >= EARLY:
+                    text_branch(*blocks[s], "late", 8 - EARLY)
                 picture_branch(*blocks[s])
                 gate_branch(*blocks[s])
                 subtract(blocks[s])

@@ -27,6 +27,7 @@ J_CHUNKS = J // JC
 NH = 256
 V_SHIFT = 4
 EARLY = 4
+STAGE = 16
 
 
 def tile_list_gmu_tanh_none_kernel(
@@ -98,9 +99,9 @@ def tile_list_gmu_tanh_none_kernel(
             )
 
         def move_t_scales():
-            for q in range(QUADS):
-                rows = s2_got[2 * ROWS * q : 2 * ROWS * (q + 1), :]
-                nc.sync.dma_start(out=t_planes[32 * q : 32 * q + ROWS, :, :], in_=rows)
+            for r in range(ROWS):
+                rows = s2_got[2 * QUADS * r : 2 * QUADS * (r + 1), :]
+                nc.sync.dma_start(out=t_planes[r:P:32, :, :], in_=rows)
 
         def load_plane(queue, plane, scales, shift):
             for r in range(ROWS):
@@ -110,10 +111,12 @@ def tile_list_gmu_tanh_none_kernel(
         def load_weight_scales(queue, first, scales):
             passes = scales.shape[0]
             rows = scales.rearrange("a q n -> q a n").bitcast(I32)
-            queue.dma_start(out=w_planes[0 : QUADS * ROWS, first : first + passes, :], in_=rows)
+            queue.dma_start(out=w_planes[STAGE : STAGE + QUADS * ROWS, first : first + passes, :], in_=rows)
 
         nc.sync.dma_start(list2[:], offs2)
-        nc.sync.dma_start(out=s2_win[0:32, :], in_=tab2_scales.rearrange("a q t -> q a t").bitcast(I32))
+        for a in range(2):
+            rows = tab2_scales[a].rearrange("(q r) t -> r q t", r=ROWS).bitcast(I32)
+            nc.sync.dma_start(out=s2_win[a:32:2, :], in_=rows)
         nc.sync.dma_start(list1[:], offs)
         nc.sync.dma_start(out=w2_win[:], in_=words(tab2_words))
         load_plane(nc.sync, s1_win, tab_scales, V_SHIFT)
@@ -133,9 +136,9 @@ def tile_list_gmu_tanh_none_kernel(
         )
         load_weight_scales(nc.sync, 0, wv_scales)
         nc.sync.dma_start(out=w1_win[:], in_=words(tab_words))
-        for q in range(1, QUADS):
+        for r in range(ROWS):
             nc.sync.dma_start(
-                out=w_planes[32 * q : 32 * q + ROWS, :, :], in_=w_planes[ROWS * q : ROWS * (q + 1), :, :]
+                out=w_planes[r:P:32, :, :], in_=w_planes[STAGE + r : STAGE + QUADS * ROWS : ROWS, :, :]
             )
         for h in range(N // NH):
             cols = slice(NH * h, NH * (h + 1))

@@ -1,6 +1,7 @@
 from contextlib import ExitStack
 
 import concourse.mybir as mybir
+from concourse.masks import make_identity
 
 K, L, N, T, J = 512, 1024, 512, 2048, 1024
 FLOPS = 2 * 2 * (K + L) * N * J
@@ -72,6 +73,8 @@ def tile_list_gmu_tanh_none_kernel(
         nc.vector.memset(s2_win[32:64, :], 0)
         nc.vector.memset(s2_win[64:128, :], 0)
         nc.gpsimd.memset(t_planes[:], 0)
+        identity = held("identity", [P, P], F32)
+        make_identity(nc, identity[:])
 
         def load_wt(k):
             a, h = k
@@ -187,23 +190,27 @@ def tile_list_gmu_tanh_none_kernel(
 
         at, av, gt, diff, mixed = {}, {}, {}, {}, {}
 
-        def text_branch(c, t, tag, bufs):
-            acc = psum.tile([P, JC], F32, name="ht", tag=tag, bufs=bufs)
+        def bank(name, first_set):
+            return psum.tile([P, JC], F32, name=name, tag="first" if first_set else "second", bufs=4)
+
+        def text_branch(c, t, order):
+            acc = bank("ht", t < 2)
             cols = slice(M * t, M * (t + 1))
-            for a in range(2):
-                t_pass(acc, wt_codes[:, a, cols].bitcast(FP8X4), wt_plane[:, a, cols], c, a, a == 0, a == 1)
+            for a in order:
+                codes = wt_codes[:, a, cols].bitcast(FP8X4)
+                t_pass(acc, codes, wt_plane[:, a, cols], c, a, a == order[0], a == order[1])
             if (c, t) not in at:
                 at[c, t] = held("at%d%d" % (c, t), [P, JC], F32)[:]
             nc.scalar.activation(out=at[c, t], in_=acc[:], func=TANH)
 
         def picture_branch(c, t):
-            acc = psum.tile([P, JC], F32, name="hv", tag="late", bufs=8 - EARLY)
+            acc = bank("hv", t >= 2)
             v_pass(acc, wv_sb, 0, c, t, True, True)
             av[c, t] = held("av%d%d" % (c, t), [P, JC], F32)
             nc.scalar.activation(out=av[c, t][:], in_=acc[:], func=TANH)
 
         def gate_branch(c, t):
-            acc = psum.tile([P, JC], F32, name="z", tag="late", bufs=8 - EARLY)
+            acc = bank("z", t >= 2)
             v_pass(acc, zv_sb, 1, c, t, True, False)
             for a in range(2):
                 codes = zt_sb[t // 2][:, a, :].bitcast(U8)[:, 2 * M * (t % 2) : 2 * M * (t % 2 + 1)].bitcast(FP4X4)
@@ -211,6 +218,61 @@ def tile_list_gmu_tanh_none_kernel(
                 t_pass(acc, codes, scale, c, a, False, a == 1)
             gt[c, t] = held("gt%d%d" % (c, t), [P, JC], F32)
             nc.scalar.activation(out=gt[c, t][:], in_=acc[:], func=TANH, bias=half_b[:, t : t + 1], scale=0.5)
+
+        def turned_text(c, t):
+            cols = slice(M * t, M * (t + 1))
+            text = bank("ht", False)
+            for u in range(JC // M):
+                for a in (1, 0):
+                    nc.tensor.matmul_mx(
+                        out=text[:, M * u : M * (u + 1)],
+                        lhsT=t_part[c][:, a, 2 * M * u : 2 * M * (u + 1)].bitcast(FP4X4),
+                        lhsT_scale=t_planes[:, a, :].bitcast(U8)[:, JC * c + M * u : JC * c + M * (u + 1)],
+                        rhs=wt_codes[:, a, cols].bitcast(FP8X4),
+                        rhs_scale=wt_plane[:, a, cols],
+                        start=a == 1,
+                        stop=a == 0,
+                    )
+            minus_at = held("minus_at", [P, JC], F32)
+            nc.scalar.activation(out=minus_at[:], in_=text[:], func=TANH, scale=-1.0)
+            return minus_at
+
+        def turned_picture(c, t):
+            cols = slice(M * t, M * (t + 1))
+            picture = bank("hv", True)
+            for u in range(JC // M):
+                nc.tensor.matmul_mx(
+                    out=picture[:, M * u : M * (u + 1)],
+                    lhsT=v_got[c][:, M * u : M * (u + 1)].bitcast(FP8X4),
+                    lhsT_scale=v_plane[V_SHIFT:, JC * c + M * u : JC * c + M * (u + 1)],
+                    rhs=wv_sb[t // 2][:, M * (t % 2) : M * (t % 2 + 1)].bitcast(FP8X4),
+                    rhs_scale=w_planes[:, 0, :].bitcast(U8)[:, cols],
+                    start=True,
+                    stop=True,
+                )
+            turned_av = held("turned_av", [P, JC], F32)
+            nc.scalar.activation(out=turned_av[:], in_=picture[:], func=TANH)
+            return turned_av
+
+        def turn_text_back(k, minus_at):
+            diff[k] = bank("diff_sum", False)
+            at[k] = bank("minus_at_back", False)[:]
+            for u in range(JC // M):
+                cols = slice(M * u, M * (u + 1))
+                nc.tensor.transpose(at[k][:, cols], minus_at[:, cols], identity[:])
+            for u in range(JC // M):
+                cols = slice(M * u, M * (u + 1))
+                nc.tensor.matmul(
+                    diff[k][:, cols], minus_at[:, cols], identity[:], start=u == 0, stop=False, is_transpose=True
+                )
+
+        def turn_picture_back(k, turned_av):
+            for u in range(JC // M):
+                cols = slice(M * u, M * (u + 1))
+                nc.tensor.matmul(
+                    diff[k][:, cols], turned_av[:, cols], identity[:],
+                    start=False, stop=u == JC // M - 1, is_transpose=True,
+                )
 
         def subtract(k):
             diff[k] = work.tile([P, JC], F32, name="diff")
@@ -232,7 +294,7 @@ def tile_list_gmu_tanh_none_kernel(
                 cols = slice(first, last)
                 nc.vector.scalar_tensor_tensor(
                     out=result[:, cols], in0=mixed[k][:, cols], scalar=0.5, in1=at[k][:, cols],
-                    op0=ALU.mult, op1=ALU.add,
+                    op0=ALU.mult, op1=ALU.subtract if k == blocks[-1] else ALU.add,
                 )
                 nc.sync.dma_start(out=out[M * t : M * (t + 1), JC * c + first : JC * c + last], in_=result[:, cols])
 
@@ -253,23 +315,33 @@ def tile_list_gmu_tanh_none_kernel(
         blocks = [(c, 2 * h + t) for h in range(2) for c in range(J_CHUNKS) for t in range(2)]
 
         def parts(s):
-            return [(0, JC // 2), (JC // 2, JC)] if s == len(blocks) - 1 else [(0, JC)]
+            return [(0, JC // 2), (JC // 2, JC)] if s >= len(blocks) - 2 else [(0, JC)]
 
         at_early = shared("at_early", "raw%d%d" % pieces[2], [P, EARLY, JC], F32)
         for s, k in enumerate(blocks[:EARLY]):
             at[k] = at_early[:, s, :]
-            text_branch(*k, "early", EARLY)
-        for s in range(len(blocks) + 2):
-            if s < len(blocks):
-                if s == 2:
-                    cast(pieces[3])
-                    quantise(pieces[3])
-                if s >= EARLY:
-                    text_branch(*blocks[s], "late", 8 - EARLY)
+            text_branch(*k, (0, 1))
+        last = len(blocks) - 1
+        for s in range(len(blocks) + 1):
+            if s == 2:
+                cast(pieces[3])
+                quantise(pieces[3])
+            if EARLY <= s < last:
+                text_branch(*blocks[s], (1, 0))
+            if s < last:
                 picture_branch(*blocks[s])
+            if s == last - 1:
+                minus_at = turned_text(*blocks[last])
+            if s == last:
+                turned_av = turned_picture(*blocks[last])
+                turn_text_back(blocks[s], minus_at)
+            if s <= last:
                 gate_branch(*blocks[s])
-                subtract(blocks[s])
-            if 2 <= s:
-                finish(blocks[s - 2], parts(s - 2))
-            if 1 <= s <= len(blocks):
+            if s == last:
+                turn_picture_back(blocks[s], turned_av)
+            if s >= 1:
                 weigh(blocks[s - 1], parts(s - 1))
+            if s < last:
+                subtract(blocks[s])
+            if s >= 1:
+                finish(blocks[s - 1], parts(s - 1))

@@ -146,8 +146,8 @@ def tile_list_gmu_tanh_none_kernel(
         for h in range(N // NH):
             cols = slice(NH * h, NH * (h + 1))
             halves = slice(NH // 2 * h, NH // 2 * (h + 1))
-            nc.sync.dma_start(out=wv_sb[h][:], in_=words(wv_words)[:, cols])
             nc.sync.dma_start(out=zt_sb[h][:], in_=zt_words.rearrange("a p n -> p a n").bitcast(I32)[:, :, halves])
+            nc.sync.dma_start(out=wv_sb[h][:], in_=words(wv_words)[:, cols])
             nc.sync.dma_start(out=zv_sb[h][:], in_=words(zv_words)[:, cols])
         load_wt(pieces[3])
 
@@ -190,11 +190,17 @@ def tile_list_gmu_tanh_none_kernel(
 
         at, av, gt, diff, mixed = {}, {}, {}, {}, {}
 
-        def bank(name, first_set):
-            return psum.tile([P, JC], F32, name=name, tag="first" if first_set else "second", bufs=4)
+        def bank(name, number):
+            return psum.tile([P, JC], F32, name=name, tag="bank%d" % number)
+
+        def picture_bank(c, t):
+            return 4 + 2 * t + c if t < 2 else 2 * (t - 2)
+
+        def text_bank(c, t):
+            return 2 * c + t if t < 2 else 5 + 2 * c - (t - 2)
 
         def text_branch(c, t, order):
-            acc = bank("ht", t < 2)
+            acc = bank("ht", text_bank(c, t))
             cols = slice(M * t, M * (t + 1))
             for a in order:
                 codes = wt_codes[:, a, cols].bitcast(FP8X4)
@@ -204,24 +210,24 @@ def tile_list_gmu_tanh_none_kernel(
             nc.scalar.activation(out=at[c, t], in_=acc[:], func=TANH)
 
         def picture_branch(c, t):
-            acc = bank("hv", t >= 2)
+            acc = bank("hv", picture_bank(c, t))
             v_pass(acc, wv_sb, 0, c, t, True, True)
             av[c, t] = held("av%d%d" % (c, t), [P, JC], F32)
             nc.scalar.activation(out=av[c, t][:], in_=acc[:], func=TANH)
 
         def gate_branch(c, t):
-            acc = bank("z", t >= 2)
-            v_pass(acc, zv_sb, 1, c, t, True, False)
+            acc = bank("z", picture_bank(c, t) ^ 1)
             for a in range(2):
                 codes = zt_sb[t // 2][:, a, :].bitcast(U8)[:, 2 * M * (t % 2) : 2 * M * (t % 2 + 1)].bitcast(FP4X4)
                 scale = w_planes[:, 2 + a, :].bitcast(U8)[:, M * t : M * (t + 1)]
-                t_pass(acc, codes, scale, c, a, False, a == 1)
+                t_pass(acc, codes, scale, c, a, a == 0, False)
+            v_pass(acc, zv_sb, 1, c, t, False, True)
             gt[c, t] = held("gt%d%d" % (c, t), [P, JC], F32)
             nc.scalar.activation(out=gt[c, t][:], in_=acc[:], func=TANH, bias=half_b[:, t : t + 1], scale=0.5)
 
         def turned_text(c, t):
             cols = slice(M * t, M * (t + 1))
-            text = bank("ht", False)
+            text = bank("ht", text_bank(c, t))
             for u in range(JC // M):
                 for a in (1, 0):
                     nc.tensor.matmul_mx(
@@ -239,7 +245,7 @@ def tile_list_gmu_tanh_none_kernel(
 
         def turned_picture(c, t):
             cols = slice(M * t, M * (t + 1))
-            picture = bank("hv", True)
+            picture = bank("hv", picture_bank(c, t))
             for u in range(JC // M):
                 nc.tensor.matmul_mx(
                     out=picture[:, M * u : M * (u + 1)],
@@ -255,8 +261,8 @@ def tile_list_gmu_tanh_none_kernel(
             return turned_av
 
         def turn_text_back(k, minus_at):
-            diff[k] = bank("diff_sum", False)
-            at[k] = bank("minus_at_back", False)[:]
+            diff[k] = bank("diff_sum", text_bank(0, 2))
+            at[k] = bank("minus_at_back", text_bank(0, 3))[:]
             for u in range(JC // M):
                 cols = slice(M * u, M * (u + 1))
                 nc.tensor.transpose(at[k][:, cols], minus_at[:, cols], identity[:])
@@ -323,7 +329,7 @@ def tile_list_gmu_tanh_none_kernel(
             text_branch(*k, (0, 1))
         last = len(blocks) - 1
         for s in range(len(blocks) + 1):
-            if s == 2:
+            if s == 3:
                 cast(pieces[3])
                 quantise(pieces[3])
             if EARLY <= s < last:

@@ -28,6 +28,11 @@ J_CHUNKS = J // JC
 NH = 256
 V_SHIFT = 4
 EARLY = 4
+TEXT_BANK = (0, 1, 2, 3, 5, 4, 7, 5)
+PICTURE_BANK = (4, 6, 5, 7, 0, 2, 6, 1)
+GATE_BANK = (5, 7, 4, 6, 1, 3, 0, 4)
+DIFF_BANK, TEXT_BACK_BANK = 3, 2
+VECTOR_COLS = 96
 STAGE = 16
 
 
@@ -90,6 +95,18 @@ def tile_list_gmu_tanh_none_kernel(
             nc.scalar.copy(
                 out=wt_bf[k][:].rearrange("p (c n) i -> p c i n", n=4),
                 in_=wt_raw[k][:].rearrange("p i (c n) -> p c i n", n=4),
+            )
+
+        def cast_shared(k):
+            wt_bf[k] = held("wt_bf%d%d" % k, [P, NH, PACK], BF16)
+            cut = NH - VECTOR_COLS
+            nc.scalar.copy(
+                out=wt_bf[k][:, :cut, :].rearrange("p (c n) i -> p c i n", n=4),
+                in_=wt_raw[k][:, :, :cut].rearrange("p i (c n) -> p c i n", n=4),
+            )
+            nc.vector.tensor_copy(
+                out=wt_bf[k][:, cut:, :].rearrange("p (c n) i -> p c i n", n=4),
+                in_=wt_raw[k][:, :, cut:].rearrange("p i (c n) -> p c i n", n=4),
             )
 
         def quantise(k):
@@ -193,14 +210,8 @@ def tile_list_gmu_tanh_none_kernel(
         def bank(name, number):
             return psum.tile([P, JC], F32, name=name, tag="bank%d" % number)
 
-        def picture_bank(c, t):
-            return 4 + 2 * t + c if t < 2 else 2 * (t - 2)
-
-        def text_bank(c, t):
-            return 2 * c + t if t < 2 else 5 + 2 * c - (t - 2)
-
         def text_branch(c, t, order):
-            acc = bank("ht", text_bank(c, t))
+            acc = bank("ht", TEXT_BANK[blocks.index((c, t))])
             cols = slice(M * t, M * (t + 1))
             for a in order:
                 codes = wt_codes[:, a, cols].bitcast(FP8X4)
@@ -210,13 +221,13 @@ def tile_list_gmu_tanh_none_kernel(
             nc.scalar.activation(out=at[c, t], in_=acc[:], func=TANH)
 
         def picture_branch(c, t):
-            acc = bank("hv", picture_bank(c, t))
+            acc = bank("hv", PICTURE_BANK[blocks.index((c, t))])
             v_pass(acc, wv_sb, 0, c, t, True, True)
             av[c, t] = held("av%d%d" % (c, t), [P, JC], F32)
             nc.scalar.activation(out=av[c, t][:], in_=acc[:], func=TANH)
 
         def gate_branch(c, t):
-            acc = bank("z", picture_bank(c, t) ^ 1)
+            acc = bank("z", GATE_BANK[blocks.index((c, t))])
             for a in range(2):
                 codes = zt_sb[t // 2][:, a, :].bitcast(U8)[:, 2 * M * (t % 2) : 2 * M * (t % 2 + 1)].bitcast(FP4X4)
                 scale = w_planes[:, 2 + a, :].bitcast(U8)[:, M * t : M * (t + 1)]
@@ -227,7 +238,7 @@ def tile_list_gmu_tanh_none_kernel(
 
         def turned_text(c, t):
             cols = slice(M * t, M * (t + 1))
-            text = bank("ht", text_bank(c, t))
+            text = bank("ht", TEXT_BANK[blocks.index((c, t))])
             for u in range(JC // M):
                 for a in (1, 0):
                     nc.tensor.matmul_mx(
@@ -245,7 +256,7 @@ def tile_list_gmu_tanh_none_kernel(
 
         def turned_picture(c, t):
             cols = slice(M * t, M * (t + 1))
-            picture = bank("hv", picture_bank(c, t))
+            picture = bank("hv", PICTURE_BANK[blocks.index((c, t))])
             for u in range(JC // M):
                 nc.tensor.matmul_mx(
                     out=picture[:, M * u : M * (u + 1)],
@@ -257,12 +268,14 @@ def tile_list_gmu_tanh_none_kernel(
                     stop=True,
                 )
             turned_av = held("turned_av", [P, JC], F32)
-            nc.scalar.activation(out=turned_av[:], in_=picture[:], func=TANH)
+            for first in (0, JC // 2):
+                half = slice(first, first + JC // 2)
+                nc.scalar.activation(out=turned_av[:, half], in_=picture[:, half], func=TANH)
             return turned_av
 
         def turn_text_back(k, minus_at):
-            diff[k] = bank("diff_sum", text_bank(0, 2))
-            at[k] = bank("minus_at_back", text_bank(0, 3))[:]
+            diff[k] = bank("diff_sum", DIFF_BANK)
+            at[k] = bank("minus_at_back", TEXT_BACK_BANK)[:]
             for u in range(JC // M):
                 cols = slice(M * u, M * (u + 1))
                 nc.tensor.transpose(at[k][:, cols], minus_at[:, cols], identity[:])
@@ -330,7 +343,7 @@ def tile_list_gmu_tanh_none_kernel(
         last = len(blocks) - 1
         for s in range(len(blocks) + 1):
             if s == 3:
-                cast(pieces[3])
+                cast_shared(pieces[3])
                 quantise(pieces[3])
             if EARLY <= s < last:
                 text_branch(*blocks[s], (1, 0))

@@ -32,7 +32,6 @@ TEXT_BANK = (0, 1, 2, 3, 5, 4, 7, 5)
 PICTURE_BANK = (4, 6, 5, 7, 0, 2, 6, 1)
 GATE_BANK = (5, 7, 4, 6, 1, 3, 0, 4)
 DIFF_BANK, TEXT_BACK_BANK = 3, 2
-VECTOR_COLS = 96
 STAGE = 16
 
 
@@ -95,18 +94,6 @@ def tile_list_gmu_tanh_none_kernel(
             nc.scalar.copy(
                 out=wt_bf[k][:].rearrange("p (c n) i -> p c i n", n=4),
                 in_=wt_raw[k][:].rearrange("p i (c n) -> p c i n", n=4),
-            )
-
-        def cast_shared(k):
-            wt_bf[k] = held("wt_bf%d%d" % k, [P, NH, PACK], BF16)
-            cut = NH - VECTOR_COLS
-            nc.scalar.copy(
-                out=wt_bf[k][:, :cut, :].rearrange("p (c n) i -> p c i n", n=4),
-                in_=wt_raw[k][:, :, :cut].rearrange("p i (c n) -> p c i n", n=4),
-            )
-            nc.vector.tensor_copy(
-                out=wt_bf[k][:, cut:, :].rearrange("p (c n) i -> p c i n", n=4),
-                in_=wt_raw[k][:, :, cut:].rearrange("p i (c n) -> p c i n", n=4),
             )
 
         def quantise(k):
@@ -343,7 +330,7 @@ def tile_list_gmu_tanh_none_kernel(
         last = len(blocks) - 1
         for s in range(len(blocks) + 1):
             if s == 3:
-                cast_shared(pieces[3])
+                cast(pieces[3])
                 quantise(pieces[3])
             if EARLY <= s < last:
                 text_branch(*blocks[s], (1, 0))

@@ -28,6 +28,7 @@ J_CHUNKS = J // JC
 NH = 256
 V_SHIFT = 4
 EARLY = 4
+PLAIN = 2
 TEXT_BANK = (0, 1, 2, 3, 5, 4, 7, 5)
 PICTURE_BANK = (4, 6, 5, 7, 0, 2, 6, 1)
 GATE_BANK = (5, 7, 4, 6, 1, 3, 0, 4)
@@ -223,6 +224,11 @@ def tile_list_gmu_tanh_none_kernel(
             gt[c, t] = held("gt%d%d" % (c, t), [P, JC], F32)
             nc.scalar.activation(out=gt[c, t][:], in_=acc[:], func=TANH, bias=half_b[:, t : t + 1], scale=0.5)
 
+        def operands(c, u, turned, table, table_scale, weights, weights_scale):
+            if turned:
+                return {"lhsT": table, "lhsT_scale": table_scale, "rhs": weights, "rhs_scale": weights_scale}
+            return {"lhsT": weights, "lhsT_scale": weights_scale, "rhs": table, "rhs_scale": table_scale}
+
         def turned_text(c, t):
             cols = slice(M * t, M * (t + 1))
             text = bank("ht", TEXT_BANK[blocks.index((c, t))])
@@ -230,12 +236,15 @@ def tile_list_gmu_tanh_none_kernel(
                 for a in (1, 0):
                     nc.tensor.matmul_mx(
                         out=text[:, M * u : M * (u + 1)],
-                        lhsT=t_part[c][:, a, 2 * M * u : 2 * M * (u + 1)].bitcast(FP4X4),
-                        lhsT_scale=t_planes[:, a, :].bitcast(U8)[:, JC * c + M * u : JC * c + M * (u + 1)],
-                        rhs=wt_codes[:, a, cols].bitcast(FP8X4),
-                        rhs_scale=wt_plane[:, a, cols],
                         start=a == 1,
                         stop=a == 0,
+                        **operands(
+                            c, u, u >= PLAIN,
+                            t_part[c][:, a, 2 * M * u : 2 * M * (u + 1)].bitcast(FP4X4),
+                            t_planes[:, a, :].bitcast(U8)[:, JC * c + M * u : JC * c + M * (u + 1)],
+                            wt_codes[:, a, cols].bitcast(FP8X4),
+                            wt_plane[:, a, cols],
+                        ),
                     )
             minus_at = held("minus_at", [P, JC], F32)
             nc.scalar.activation(out=minus_at[:], in_=text[:], func=TANH, scale=-1.0)
@@ -247,38 +256,60 @@ def tile_list_gmu_tanh_none_kernel(
             for u in range(JC // M):
                 nc.tensor.matmul_mx(
                     out=picture[:, M * u : M * (u + 1)],
-                    lhsT=v_got[c][:, M * u : M * (u + 1)].bitcast(FP8X4),
-                    lhsT_scale=v_plane[V_SHIFT:, JC * c + M * u : JC * c + M * (u + 1)],
-                    rhs=wv_sb[t // 2][:, M * (t % 2) : M * (t % 2 + 1)].bitcast(FP8X4),
-                    rhs_scale=w_planes[:, 0, :].bitcast(U8)[:, cols],
                     start=True,
                     stop=True,
+                    **operands(
+                        c, u, u >= PLAIN,
+                        v_got[c][:, M * u : M * (u + 1)].bitcast(FP8X4),
+                        v_plane[V_SHIFT:, JC * c + M * u : JC * c + M * (u + 1)],
+                        wv_sb[t // 2][:, M * (t % 2) : M * (t % 2 + 1)].bitcast(FP8X4),
+                        w_planes[:, 0, :].bitcast(U8)[:, cols],
+                    ),
                 )
             turned_av = held("turned_av", [P, JC], F32)
-            for first in (0, JC // 2):
-                half = slice(first, first + JC // 2)
+            for half in (slice(M * PLAIN, JC), slice(0, M * PLAIN)):
                 nc.scalar.activation(out=turned_av[:, half], in_=picture[:, half], func=TANH)
             return turned_av
 
-        def turn_text_back(k, minus_at):
-            diff[k] = bank("diff_sum", DIFF_BANK)
-            at[k] = bank("minus_at_back", TEXT_BACK_BANK)[:]
-            for u in range(JC // M):
+        def turn_text_back(minus_at):
+            diff_sum = bank("diff_sum", DIFF_BANK)
+            back = bank("minus_at_back", TEXT_BACK_BANK)
+            for u in range(PLAIN, JC // M):
                 cols = slice(M * u, M * (u + 1))
-                nc.tensor.transpose(at[k][:, cols], minus_at[:, cols], identity[:])
-            for u in range(JC // M):
+                nc.tensor.transpose(back[:, cols], minus_at[:, cols], identity[:])
+            for u in range(PLAIN, JC // M):
                 cols = slice(M * u, M * (u + 1))
                 nc.tensor.matmul(
-                    diff[k][:, cols], minus_at[:, cols], identity[:], start=u == 0, stop=False, is_transpose=True
+                    diff_sum[:, cols], minus_at[:, cols], identity[:], start=u == PLAIN, stop=False, is_transpose=True
                 )
+            return diff_sum, back
 
-        def turn_picture_back(k, turned_av):
-            for u in range(JC // M):
+        def turn_picture_back(diff_sum, turned_av):
+            for u in range(PLAIN, JC // M):
                 cols = slice(M * u, M * (u + 1))
                 nc.tensor.matmul(
-                    diff[k][:, cols], turned_av[:, cols], identity[:],
+                    diff_sum[:, cols], turned_av[:, cols], identity[:],
                     start=False, stop=u == JC // M - 1, is_transpose=True,
                 )
+
+        def last_steps(k, turned_av, minus_at, diff_sum, back):
+            c, t = k
+            plain, turned = slice(0, M * PLAIN), slice(M * PLAIN, JC)
+            halves = ((plain, diff[k], minus_at), (turned, diff_sum, back))
+            mixed[k] = work.tile([P, JC], F32, name="mixed")
+            result = held("result%d%d" % k, [P, JC], F32)
+            for cols, difference, minus in halves:
+                nc.vector.scalar_tensor_tensor(
+                    out=mixed[k][:, cols], in0=gt[k][:, cols], scalar=1.0, in1=difference[:, cols],
+                    op0=ALU.add, op1=ALU.mult,
+                )
+            for cols, difference, minus in halves:
+                nc.vector.scalar_tensor_tensor(
+                    out=result[:, cols], in0=mixed[k][:, cols], scalar=0.5, in1=minus[:, cols],
+                    op0=ALU.mult, op1=ALU.subtract,
+                )
+                rows = out[M * t : M * (t + 1), JC * c + cols.start : JC * c + cols.stop]
+                nc.sync.dma_start(out=rows, in_=result[:, cols])
 
         def subtract(k):
             diff[k] = work.tile([P, JC], F32, name="diff")
@@ -300,7 +331,7 @@ def tile_list_gmu_tanh_none_kernel(
                 cols = slice(first, last)
                 nc.vector.scalar_tensor_tensor(
                     out=result[:, cols], in0=mixed[k][:, cols], scalar=0.5, in1=at[k][:, cols],
-                    op0=ALU.mult, op1=ALU.subtract if k == blocks[-1] else ALU.add,
+                    op0=ALU.mult, op1=ALU.add,
                 )
                 nc.sync.dma_start(out=out[M * t : M * (t + 1), JC * c + first : JC * c + last], in_=result[:, cols])
 
@@ -320,34 +351,36 @@ def tile_list_gmu_tanh_none_kernel(
         gather_v(1)
         blocks = [(c, 2 * h + t) for h in range(2) for c in range(J_CHUNKS) for t in range(2)]
 
-        def parts(s):
-            return [(0, JC // 2), (JC // 2, JC)] if s >= len(blocks) - 2 else [(0, JC)]
-
         at_early = shared("at_early", "raw%d%d" % pieces[2], [P, EARLY, JC], F32)
         for s, k in enumerate(blocks[:EARLY]):
             at[k] = at_early[:, s, :]
             text_branch(*k, (0, 1))
         last = len(blocks) - 1
-        for s in range(len(blocks) + 1):
+        whole = [(0, JC)]
+        for s in range(last):
             if s == 3:
                 cast(pieces[3])
                 quantise(pieces[3])
-            if EARLY <= s < last:
+            if s >= EARLY:
                 text_branch(*blocks[s], (1, 0))
-            if s < last:
-                picture_branch(*blocks[s])
+            picture_branch(*blocks[s])
             if s == last - 1:
                 minus_at = turned_text(*blocks[last])
-            if s == last:
-                turned_av = turned_picture(*blocks[last])
-                turn_text_back(blocks[s], minus_at)
-            if s <= last:
-                gate_branch(*blocks[s])
-            if s == last:
-                turn_picture_back(blocks[s], turned_av)
+            gate_branch(*blocks[s])
             if s >= 1:
-                weigh(blocks[s - 1], parts(s - 1))
-            if s < last:
-                subtract(blocks[s])
+                weigh(blocks[s - 1], whole)
+            subtract(blocks[s])
             if s >= 1:
-                finish(blocks[s - 1], parts(s - 1))
+                finish(blocks[s - 1], whole)
+        k = blocks[last]
+        turned_av = turned_picture(*k)
+        diff_sum, back = turn_text_back(minus_at)
+        gate_branch(*k)
+        turn_picture_back(diff_sum, turned_av)
+        weigh(blocks[last - 1], whole)
+        diff[k] = work.tile([P, JC], F32, name="diff")
+        nc.vector.tensor_tensor(
+            out=diff[k][:, : M * PLAIN], in0=turned_av[:, : M * PLAIN], in1=minus_at[:, : M * PLAIN], op=ALU.add
+        )
+        finish(blocks[last - 1], whole)
+        last_steps(k, turned_av, minus_at, diff_sum, back)

@@ -64,7 +64,6 @@ def tile_list_gmu_tanh_none_kernel(
         zv_sb = [held("zv_sb%d" % h, [P, NH], I32) for h in range(N // NH)]
         zt_sb = [held("zt_sb%d" % h, [P, 2, NH // 2], I32) for h in range(N // NH)]
         w2_win = held("w2_win", [P, T], I32)
-        half_b = held("half_b", [P, N_TILES], F32)
         wt_codes = held("wt_codes", [P, 2, N], U32)
         wt_plane = held("wt_plane", [P, 2, N], U8)
         pieces = [(a, h) for h in range(N // NH) for a in range(2)]
@@ -91,10 +90,17 @@ def tile_list_gmu_tanh_none_kernel(
             return ap[0].rearrange("p n i -> p (n i)").bitcast(I32)
 
         def cast(k):
-            wt_bf[k] = held("wt_bf%d%d" % k, [P, NH, PACK], BF16)
+            wt_bf[k] = shared("wt_bf%d%d" % k, "wt_bf%d%d" % k, [P, NH, PACK], BF16)
             nc.scalar.copy(
                 out=wt_bf[k][:].rearrange("p (c n) i -> p c i n", n=4),
                 in_=wt_raw[k][:].rearrange("p i (c n) -> p c i n", n=4),
+            )
+
+        def cast_beside_gather(k, after):
+            wt_bf[k] = shared("wt_bf%d%d" % k, "wt_bf%d%d" % after, [P, NH, PACK], BF16)
+            nc.gpsimd.tensor_scalar(
+                out=wt_bf[k][:], in0=wt_raw[k][:].rearrange("p i n -> p n i"),
+                scalar1=1.0, scalar2=0.0, op0=ALU.mult, op1=ALU.add,
             )
 
         def quantise(k):
@@ -139,9 +145,6 @@ def tile_list_gmu_tanh_none_kernel(
         b_sb = shared("b_sb", "early", [P, N_TILES], F32)
         with nc.allow_non_contiguous_dma(reason="one bias value for each partition"):
             nc.gpsimd.dma_start(out=b_sb[:], in_=b.rearrange("(c p) -> p c", p=P))
-        nc.gpsimd.tensor_scalar(
-            out=half_b[:], in0=b_sb[:], scalar1=0.5, scalar2=0.0, op0=ALU.mult, op1=ALU.add
-        )
         load_weight_scales(nc.sync, 0, wv_scales)
         nc.sync.dma_start(out=w1_win[:], in_=words(tab_words))
         for r in range(ROWS):
@@ -345,13 +348,17 @@ def tile_list_gmu_tanh_none_kernel(
         quantise(pieces[1])
         v_plane = shared("v_plane", "raw%d%d" % pieces[1], [P, J], U8)
         nc.vector.tensor_copy(out=v_plane[:], in_=s1_win[:].bitcast(U8).indirect(list1[:]))
-        cast(pieces[2])
+        cast_beside_gather(pieces[2], pieces[1])
+        half_b = shared("half_b", "raw%d%d" % pieces[2], [P, N_TILES], F32)
+        nc.gpsimd.tensor_scalar(
+            out=half_b[:], in0=b_sb[:], scalar1=0.5, scalar2=0.0, op0=ALU.mult, op1=ALU.add
+        )
         quantise(pieces[2])
         gather_v(0)
         gather_v(1)
         blocks = [(c, 2 * h + t) for h in range(2) for c in range(J_CHUNKS) for t in range(2)]
 
-        at_early = shared("at_early", "raw%d%d" % pieces[2], [P, EARLY, JC], F32)
+        at_early = held("at_early", [P, EARLY, JC], F32)
         for s, k in enumerate(blocks[:EARLY]):
             at[k] = at_early[:, s, :]
             text_branch(*k, (0, 1))

@@ -28,11 +28,12 @@ J_CHUNKS = J // JC
 NH = 256
 V_SHIFT = 4
 EARLY = 4
-PLAIN = 2
-TEXT_BANK = (0, 1, 2, 3, 5, 4, 7, 5)
-PICTURE_BANK = (4, 6, 5, 7, 0, 2, 6, 1)
-GATE_BANK = (5, 7, 4, 6, 1, 3, 0, 4)
-DIFF_BANK, TEXT_BACK_BANK = 3, 2
+PLAIN_BLOCKS = 6
+TEXT_BANK = (0, 1, 2, 3, 5, 4, 7, 6)
+PICTURE_BANK = (4, 6, 5, 7, 0, 2, 5, 0)
+GATE_BANK = (5, 7, 4, 6, 1, 3, 1, 4)
+DIFF_BANK = (2, 3)
+BACK_BANK = (7, 6)
 STAGE = 16
 
 
@@ -89,18 +90,11 @@ def tile_list_gmu_tanh_none_kernel(
         def words(ap):
             return ap[0].rearrange("p n i -> p (n i)").bitcast(I32)
 
-        def cast(k):
+        def cast(copy, k):
             wt_bf[k] = shared("wt_bf%d%d" % k, "wt_bf%d%d" % k, [P, NH, PACK], BF16)
-            nc.scalar.copy(
+            copy(
                 out=wt_bf[k][:].rearrange("p (c n) i -> p c i n", n=4),
                 in_=wt_raw[k][:].rearrange("p i (c n) -> p c i n", n=4),
-            )
-
-        def cast_beside_gather(k, after):
-            wt_bf[k] = shared("wt_bf%d%d" % k, "wt_bf%d%d" % after, [P, NH, PACK], BF16)
-            nc.gpsimd.tensor_scalar(
-                out=wt_bf[k][:], in0=wt_raw[k][:].rearrange("p i n -> p n i"),
-                scalar1=1.0, scalar2=0.0, op0=ALU.mult, op1=ALU.add,
             )
 
         def quantise(k):
@@ -141,23 +135,35 @@ def tile_list_gmu_tanh_none_kernel(
 
         nc.vector.tensor_copy(out=s2_got[:].bitcast(U8), in_=s2_win[:].bitcast(U8).indirect(list2[:]))
         move_t_scales()
-        load_wt(pieces[2])
         b_sb = shared("b_sb", "early", [P, N_TILES], F32)
         with nc.allow_non_contiguous_dma(reason="one bias value for each partition"):
             nc.gpsimd.dma_start(out=b_sb[:], in_=b.rearrange("(c p) -> p c", p=P))
+        half_b = held("half_b", [P, N_TILES], F32)
+        nc.gpsimd.tensor_scalar(
+            out=half_b[:], in0=b_sb[:], scalar1=0.5, scalar2=0.0, op0=ALU.mult, op1=ALU.add
+        )
+
+        def load_zt(h):
+            halves = slice(NH // 2 * h, NH // 2 * (h + 1))
+            nc.sync.dma_start(out=zt_sb[h][:], in_=zt_words.rearrange("a p n -> p a n").bitcast(I32)[:, :, halves])
+
+        def load_v_weights(h):
+            cols = slice(NH * h, NH * (h + 1))
+            nc.sync.dma_start(out=wv_sb[h][:], in_=words(wv_words)[:, cols])
+            nc.sync.dma_start(out=zv_sb[h][:], in_=words(zv_words)[:, cols])
+
         load_weight_scales(nc.sync, 0, wv_scales)
+        load_zt(0)
         nc.sync.dma_start(out=w1_win[:], in_=words(tab_words))
         for r in range(ROWS):
             nc.sync.dma_start(
                 out=w_planes[r:P:32, :, :], in_=w_planes[STAGE + r : STAGE + QUADS * ROWS : ROWS, :, :]
             )
-        for h in range(N // NH):
-            cols = slice(NH * h, NH * (h + 1))
-            halves = slice(NH // 2 * h, NH // 2 * (h + 1))
-            nc.sync.dma_start(out=zt_sb[h][:], in_=zt_words.rearrange("a p n -> p a n").bitcast(I32)[:, :, halves])
-            nc.sync.dma_start(out=wv_sb[h][:], in_=words(wv_words)[:, cols])
-            nc.sync.dma_start(out=zv_sb[h][:], in_=words(zv_words)[:, cols])
+        load_v_weights(0)
+        load_wt(pieces[2])
         load_wt(pieces[3])
+        load_zt(1)
+        load_v_weights(1)
 
         def entries(lst, c):
             return lst[:, c * JC // 16 : (c + 1) * JC // 16]
@@ -227,133 +233,88 @@ def tile_list_gmu_tanh_none_kernel(
             gt[c, t] = held("gt%d%d" % (c, t), [P, JC], F32)
             nc.scalar.activation(out=gt[c, t][:], in_=acc[:], func=TANH, bias=half_b[:, t : t + 1], scale=0.5)
 
-        def operands(c, u, turned, table, table_scale, weights, weights_scale):
-            if turned:
-                return {"lhsT": table, "lhsT_scale": table_scale, "rhs": weights, "rhs_scale": weights_scale}
-            return {"lhsT": weights, "lhsT_scale": weights_scale, "rhs": table, "rhs_scale": table_scale}
-
-        def turned_text(c, t):
-            cols = slice(M * t, M * (t + 1))
-            text = bank("ht", TEXT_BANK[blocks.index((c, t))])
-            for u in range(JC // M):
+        def turned_text(c, h, pair):
+            acc = bank("ht", TEXT_BANK[PLAIN_BLOCKS + pair])
+            for side in range(2):
+                u = 2 * pair + side
                 for a in (1, 0):
                     nc.tensor.matmul_mx(
-                        out=text[:, M * u : M * (u + 1)],
+                        out=acc[:, NH * side : NH * (side + 1)],
+                        lhsT=t_part[c][:, a, 2 * M * u : 2 * M * (u + 1)].bitcast(FP4X4),
+                        lhsT_scale=t_planes[:, a, :].bitcast(U8)[:, JC * c + M * u : JC * c + M * (u + 1)],
+                        rhs=wt_codes[:, a, NH * h : NH * (h + 1)].bitcast(FP8X4),
+                        rhs_scale=wt_plane[:, a, NH * h : NH * (h + 1)],
                         start=a == 1,
                         stop=a == 0,
-                        **operands(
-                            c, u, u >= PLAIN,
-                            t_part[c][:, a, 2 * M * u : 2 * M * (u + 1)].bitcast(FP4X4),
-                            t_planes[:, a, :].bitcast(U8)[:, JC * c + M * u : JC * c + M * (u + 1)],
-                            wt_codes[:, a, cols].bitcast(FP8X4),
-                            wt_plane[:, a, cols],
-                        ),
                     )
-            minus_at = held("minus_at", [P, JC], F32)
-            nc.scalar.activation(out=minus_at[:], in_=text[:], func=TANH, scale=-1.0)
-            return minus_at
+            minus_at[pair] = held("minus_at%d" % pair, [P, 2, NH], F32)
+            nc.scalar.activation(
+                out=minus_at[pair][:].rearrange("p s n -> p (s n)"), in_=acc[:], func=TANH, scale=-1.0
+            )
 
-        def turned_picture(c, t):
-            cols = slice(M * t, M * (t + 1))
-            picture = bank("hv", PICTURE_BANK[blocks.index((c, t))])
-            for u in range(JC // M):
+        def turned_picture(c, h, pair):
+            acc = bank("hv", PICTURE_BANK[PLAIN_BLOCKS + pair])
+            for side in range(2):
+                u = 2 * pair + side
                 nc.tensor.matmul_mx(
-                    out=picture[:, M * u : M * (u + 1)],
+                    out=acc[:, NH * side : NH * (side + 1)],
+                    lhsT=v_got[c][:, M * u : M * (u + 1)].bitcast(FP8X4),
+                    lhsT_scale=v_plane[V_SHIFT:, JC * c + M * u : JC * c + M * (u + 1)],
+                    rhs=wv_sb[h][:].bitcast(FP8X4),
+                    rhs_scale=w_planes[:, 0, :].bitcast(U8)[:, NH * h : NH * (h + 1)],
                     start=True,
                     stop=True,
-                    **operands(
-                        c, u, u >= PLAIN,
-                        v_got[c][:, M * u : M * (u + 1)].bitcast(FP8X4),
-                        v_plane[V_SHIFT:, JC * c + M * u : JC * c + M * (u + 1)],
-                        wv_sb[t // 2][:, M * (t % 2) : M * (t % 2 + 1)].bitcast(FP8X4),
-                        w_planes[:, 0, :].bitcast(U8)[:, cols],
-                    ),
                 )
-            turned_av = held("turned_av", [P, JC], F32)
-            for half in (slice(M * PLAIN, JC), slice(0, M * PLAIN)):
-                nc.scalar.activation(out=turned_av[:, half], in_=picture[:, half], func=TANH)
-            return turned_av
+            turned_av[pair] = held("turned_av%d" % pair, [P, 2, NH], F32)
+            nc.scalar.activation(out=turned_av[pair][:].rearrange("p s n -> p (s n)"), in_=acc[:], func=TANH)
 
-        def turn_text_back(minus_at):
-            diff_sum = bank("diff_sum", DIFF_BANK)
-            back = bank("minus_at_back", TEXT_BACK_BANK)
-            for u in range(PLAIN, JC // M):
-                cols = slice(M * u, M * (u + 1))
-                nc.tensor.transpose(back[:, cols], minus_at[:, cols], identity[:])
-            for u in range(PLAIN, JC // M):
-                cols = slice(M * u, M * (u + 1))
+        def turn_into_difference(k, half, source, opens):
+            if opens:
+                diff[k] = bank("diff_sum", DIFF_BANK[half])
+            for u in range(JC // M):
                 nc.tensor.matmul(
-                    diff_sum[:, cols], minus_at[:, cols], identity[:], start=u == PLAIN, stop=False, is_transpose=True
-                )
-            return diff_sum, back
-
-        def turn_picture_back(diff_sum, turned_av):
-            for u in range(PLAIN, JC // M):
-                cols = slice(M * u, M * (u + 1))
-                nc.tensor.matmul(
-                    diff_sum[:, cols], turned_av[:, cols], identity[:],
-                    start=False, stop=u == JC // M - 1, is_transpose=True,
+                    diff[k][:, M * u : M * (u + 1)], source[u // 2][:, u % 2, M * half : M * (half + 1)], identity[:],
+                    start=opens and u == 0, stop=not opens and u == JC // M - 1, is_transpose=True,
                 )
 
-        def last_steps(k, turned_av, minus_at, diff_sum, back):
-            c, t = k
-            plain, turned = slice(0, M * PLAIN), slice(M * PLAIN, JC)
-            halves = ((plain, diff[k], minus_at), (turned, diff_sum, back))
-            mixed[k] = work.tile([P, JC], F32, name="mixed")
-            result = held("result%d%d" % k, [P, JC], F32)
-            for cols, difference, minus in halves:
-                nc.vector.scalar_tensor_tensor(
-                    out=mixed[k][:, cols], in0=gt[k][:, cols], scalar=1.0, in1=difference[:, cols],
-                    op0=ALU.add, op1=ALU.mult,
+        def turn_text(k, half):
+            back[k] = bank("minus_at_back", BACK_BANK[half])
+            for u in range(JC // M):
+                nc.tensor.transpose(
+                    back[k][:, M * u : M * (u + 1)], minus_at[u // 2][:, u % 2, M * half : M * (half + 1)], identity[:]
                 )
-            for cols, difference, minus in halves:
-                nc.vector.scalar_tensor_tensor(
-                    out=result[:, cols], in0=mixed[k][:, cols], scalar=0.5, in1=minus[:, cols],
-                    op0=ALU.mult, op1=ALU.subtract,
-                )
-                rows = out[M * t : M * (t + 1), JC * c + cols.start : JC * c + cols.stop]
-                nc.sync.dma_start(out=rows, in_=result[:, cols])
 
         def subtract(k):
             diff[k] = work.tile([P, JC], F32, name="diff")
             nc.vector.tensor_tensor(out=diff[k][:], in0=av[k][:], in1=at[k], op=ALU.subtract)
 
-        def weigh(k, parts):
-            mixed[k] = work.tile([P, JC], F32, name="mixed")
-            for first, last in parts:
-                cols = slice(first, last)
-                nc.vector.scalar_tensor_tensor(
-                    out=mixed[k][:, cols], in0=gt[k][:, cols], scalar=1.0, in1=diff[k][:, cols],
-                    op0=ALU.add, op1=ALU.mult,
-                )
+        def weigh(k):
+            mixed[k] = held("mixed%d%d" % k, [P, JC], F32)
+            nc.vector.scalar_tensor_tensor(
+                out=mixed[k][:], in0=gt[k][:], scalar=1.0, in1=diff[k][:], op0=ALU.add, op1=ALU.mult
+            )
 
-        def finish(k, parts):
+        def finish(k, text, op, parts):
             c, t = k
             result = held("result%d%d" % k, [P, JC], F32)
             for first, last in parts:
                 cols = slice(first, last)
                 nc.vector.scalar_tensor_tensor(
-                    out=result[:, cols], in0=mixed[k][:, cols], scalar=0.5, in1=at[k][:, cols],
-                    op0=ALU.mult, op1=ALU.add,
+                    out=result[:, cols], in0=mixed[k][:, cols], scalar=0.5, in1=text[:, cols], op0=ALU.mult, op1=op
                 )
                 nc.sync.dma_start(out=out[M * t : M * (t + 1), JC * c + first : JC * c + last], in_=result[:, cols])
 
+        minus_at, turned_av, back = {}, {}, {}
         for c in range(J_CHUNKS):
             gather_t(c)
         part_t(0, "t_part0")
-        cast(pieces[0])
+        cast(nc.scalar.copy, pieces[0])
         quantise(pieces[0])
         part_t(1, "raw%d%d" % pieces[0])
-        cast(pieces[1])
+        cast(nc.scalar.copy, pieces[1])
         quantise(pieces[1])
         v_plane = shared("v_plane", "raw%d%d" % pieces[1], [P, J], U8)
         nc.vector.tensor_copy(out=v_plane[:], in_=s1_win[:].bitcast(U8).indirect(list1[:]))
-        cast_beside_gather(pieces[2], pieces[1])
-        half_b = shared("half_b", "raw%d%d" % pieces[2], [P, N_TILES], F32)
-        nc.gpsimd.tensor_scalar(
-            out=half_b[:], in0=b_sb[:], scalar1=0.5, scalar2=0.0, op0=ALU.mult, op1=ALU.add
-        )
-        quantise(pieces[2])
         gather_v(0)
         gather_v(1)
         blocks = [(c, 2 * h + t) for h in range(2) for c in range(J_CHUNKS) for t in range(2)]
@@ -362,32 +323,42 @@ def tile_list_gmu_tanh_none_kernel(
         for s, k in enumerate(blocks[:EARLY]):
             at[k] = at_early[:, s, :]
             text_branch(*k, (0, 1))
-        last = len(blocks) - 1
         whole = [(0, JC)]
-        for s in range(last):
-            if s == 3:
-                cast(pieces[3])
+        halves = [(0, JC // 2), (JC // 2, JC)]
+        for s in range(PLAIN_BLOCKS):
+            if s == 2:
+                cast(nc.scalar.copy, pieces[3])
+                quantise(pieces[2])
                 quantise(pieces[3])
             if s >= EARLY:
                 text_branch(*blocks[s], (1, 0))
             picture_branch(*blocks[s])
-            if s == last - 1:
-                minus_at = turned_text(*blocks[last])
             gate_branch(*blocks[s])
-            if s >= 1:
-                weigh(blocks[s - 1], whole)
+            if 1 <= s < PLAIN_BLOCKS - 1:
+                weigh(blocks[s - 1])
             subtract(blocks[s])
-            if s >= 1:
-                finish(blocks[s - 1], whole)
-        k = blocks[last]
-        turned_av = turned_picture(*k)
-        diff_sum, back = turn_text_back(minus_at)
-        gate_branch(*k)
-        turn_picture_back(diff_sum, turned_av)
-        weigh(blocks[last - 1], whole)
-        diff[k] = work.tile([P, JC], F32, name="diff")
-        nc.vector.tensor_tensor(
-            out=diff[k][:, : M * PLAIN], in0=turned_av[:, : M * PLAIN], in1=minus_at[:, : M * PLAIN], op=ALU.add
-        )
-        finish(blocks[last - 1], whole)
-        last_steps(k, turned_av, minus_at, diff_sum, back)
+            if s == 1:
+                cast(nc.vector.tensor_copy, pieces[2])
+            if 1 <= s < PLAIN_BLOCKS - 1:
+                finish(blocks[s - 1], at[blocks[s - 1]], ALU.add, whole)
+        turned = blocks[PLAIN_BLOCKS:]
+        for pair in range(2):
+            turned_text(1, 1, pair)
+        for pair in range(2):
+            turned_picture(1, 1, pair)
+        for k in turned:
+            gate_branch(*k)
+        for half, k in enumerate(turned):
+            turn_into_difference(k, half, minus_at, True)
+        turn_text(turned[0], 0)
+        for half, k in enumerate(turned):
+            turn_into_difference(k, half, turned_av, False)
+        turn_text(turned[1], 1)
+        for k in blocks[PLAIN_BLOCKS - 2 : PLAIN_BLOCKS]:
+            weigh(k)
+        for k in blocks[PLAIN_BLOCKS - 2 : PLAIN_BLOCKS]:
+            finish(k, at[k], ALU.add, whole)
+        for k in turned:
+            weigh(k)
+        finish(turned[0], back[turned[0]], ALU.subtract, whole)
+        finish(turned[1], back[turned[1]], ALU.subtract, halves)

@@ -111,8 +111,8 @@ def tile_list_gmu_tanh_none_kernel(
                 rows = s2_got[2 * QUADS * r : 2 * QUADS * (r + 1), :]
                 nc.sync.dma_start(out=t_planes[r:P:32, :, :], in_=rows)
 
-        def load_plane(queue, plane, scales, shift):
-            for r in range(ROWS):
+        def load_plane(queue, plane, scales, shift, which):
+            for r in which:
                 rows = scales[0, r::ROWS, :]
                 queue.dma_start(out=plane[shift + r : P : 32, :], in_=rows.bitcast(I32))
 
@@ -127,14 +127,16 @@ def tile_list_gmu_tanh_none_kernel(
             nc.sync.dma_start(out=s2_win[a:32:2, :], in_=rows)
         nc.sync.dma_start(list1[:], offs)
         nc.sync.dma_start(out=w2_win[:], in_=words(tab2_words))
-        load_plane(nc.sync, s1_win, tab_scales, V_SHIFT)
+        load_plane(nc.sync, s1_win, tab_scales, V_SHIFT, (0, 1))
         load_weight_scales(nc.sync, 2, zt_scales)
+        load_weight_scales(nc.sync, 0, wv_scales)
         load_weight_scales(nc.gpsimd, 1, zv_scales)
         for k in pieces[:2]:
             load_wt(k)
 
         nc.vector.tensor_copy(out=s2_got[:].bitcast(U8), in_=s2_win[:].bitcast(U8).indirect(list2[:]))
         move_t_scales()
+        load_plane(nc.sync, s1_win, tab_scales, V_SHIFT, (2, 3))
         b_sb = shared("b_sb", "early", [P, N_TILES], F32)
         with nc.allow_non_contiguous_dma(reason="one bias value for each partition"):
             nc.gpsimd.dma_start(out=b_sb[:], in_=b.rearrange("(c p) -> p c", p=P))
@@ -152,9 +154,8 @@ def tile_list_gmu_tanh_none_kernel(
             nc.sync.dma_start(out=wv_sb[h][:], in_=words(wv_words)[:, cols])
             nc.sync.dma_start(out=zv_sb[h][:], in_=words(zv_words)[:, cols])
 
-        load_weight_scales(nc.sync, 0, wv_scales)
-        load_zt(0)
         nc.sync.dma_start(out=w1_win[:], in_=words(tab_words))
+        load_zt(0)
         for r in range(ROWS):
             nc.sync.dma_start(
                 out=w_planes[r:P:32, :, :], in_=w_planes[STAGE + r : STAGE + QUADS * ROWS : ROWS, :, :]

@@ -29,12 +29,15 @@ NH = 256
 V_SHIFT = 4
 EARLY = 4
 PLAIN_BLOCKS = 6
-TEXT_BANK = (0, 1, 2, 3, 5, 4, 7, 6)
-PICTURE_BANK = (4, 6, 5, 7, 0, 2, 5, 0)
-GATE_BANK = (5, 7, 4, 6, 1, 3, 1, 4)
+EARLY_GATES = 3
+TEXT_BANK = (0, 1, 2, 3, 5, 0, 7, 6)
+PICTURE_BANK = (4, 6, 5, 7, 4, 2, 5, 4)
+GATE_BANK = (5, 7, 0, 6, 1, 3, 1, 0)
 DIFF_BANK = (2, 3)
 BACK_BANK = (7, 6)
 STAGE = 16
+WARM_UP_PASSES = 4
+WARM_UP_BANK = 4
 
 
 def tile_list_gmu_tanh_none_kernel(
@@ -203,7 +206,7 @@ def tile_list_gmu_tanh_none_kernel(
                 stop=stop,
             )
 
-        at, av, gt, diff, mixed = {}, {}, {}, {}, {}
+        at, av, gt, diff, mixed, z_sum = {}, {}, {}, {}, {}, {}
 
         def bank(name, number):
             return psum.tile([P, JC], F32, name=name, tag="bank%d" % number)
@@ -224,12 +227,17 @@ def tile_list_gmu_tanh_none_kernel(
             av[c, t] = held("av%d%d" % (c, t), [P, JC], F32)
             nc.scalar.activation(out=av[c, t][:], in_=acc[:], func=TANH)
 
-        def gate_branch(c, t):
-            acc = bank("z", GATE_BANK[blocks.index((c, t))])
+        def open_gate(c, t):
+            acc = z_sum[c, t] = bank("z", GATE_BANK[blocks.index((c, t))])
             for a in range(2):
                 codes = zt_sb[t // 2][:, a, :].bitcast(U8)[:, 2 * M * (t % 2) : 2 * M * (t % 2 + 1)].bitcast(FP4X4)
                 scale = w_planes[:, 2 + a, :].bitcast(U8)[:, M * t : M * (t + 1)]
                 t_pass(acc, codes, scale, c, a, a == 0, False)
+
+        def gate_branch(c, t):
+            if (c, t) not in z_sum:
+                open_gate(c, t)
+            acc = z_sum[c, t]
             v_pass(acc, zv_sb, 1, c, t, False, True)
             gt[c, t] = held("gt%d%d" % (c, t), [P, JC], F32)
             nc.scalar.activation(out=gt[c, t][:], in_=acc[:], func=TANH, bias=half_b[:, t : t + 1], scale=0.5)
@@ -308,6 +316,17 @@ def tile_list_gmu_tanh_none_kernel(
         minus_at, turned_av, back = {}, {}, {}
         for c in range(J_CHUNKS):
             gather_t(c)
+        warm = bank("warm", WARM_UP_BANK)
+        for repeat in range(WARM_UP_PASSES):
+            nc.tensor.matmul_mx(
+                out=warm[:],
+                lhsT=t_got[0][:].bitcast(U8)[:, : 2 * M].bitcast(FP4X4),
+                lhsT_scale=s2_got[:].bitcast(U8)[:, :M],
+                rhs=t_got[0][:].bitcast(U8)[:, : 2 * JC].bitcast(FP4X4),
+                rhs_scale=s2_got[:].bitcast(U8)[:, :JC],
+                start=True,
+                stop=True,
+            )
         part_t(0, "t_part0")
         cast(nc.scalar.copy, pieces[0])
         quantise(pieces[0])
@@ -324,6 +343,8 @@ def tile_list_gmu_tanh_none_kernel(
         for s, k in enumerate(blocks[:EARLY]):
             at[k] = at_early[:, s, :]
             text_branch(*k, (0, 1))
+        for k in blocks[:EARLY_GATES]:
+            open_gate(*k)
         whole = [(0, JC)]
         halves = [(0, JC // 2), (JC // 2, JC)]
         for s in range(PLAIN_BLOCKS):

@@ -33,8 +33,8 @@ EARLY_GATES = 3
 TEXT_BANK = (0, 1, 2, 3, 5, 0, 7, 6)
 PICTURE_BANK = (4, 6, 5, 7, 4, 2, 5, 4)
 GATE_BANK = (5, 7, 0, 6, 1, 3, 1, 0)
-DIFF_BANK = (2, 3)
-BACK_BANK = (7, 6)
+DIFF_BANK = (2, 7)
+BACK_BANK = (3, 5)
 STAGE = 16
 WARM_UP_PASSES = 4
 WARM_UP_BANK = 4
@@ -277,20 +277,69 @@ def tile_list_gmu_tanh_none_kernel(
             turned_av[pair] = held("turned_av%d" % pair, [P, 2, NH], F32)
             nc.scalar.activation(out=turned_av[pair][:].rearrange("p s n -> p (s n)"), in_=acc[:], func=TANH)
 
-        def turn_into_difference(k, half, source, opens):
-            if opens:
-                diff[k] = bank("diff_sum", DIFF_BANK[half])
-            for u in range(JC // M):
-                nc.tensor.matmul(
-                    diff[k][:, M * u : M * (u + 1)], source[u // 2][:, u % 2, M * half : M * (half + 1)], identity[:],
-                    start=opens and u == 0, stop=not opens and u == JC // M - 1, is_transpose=True,
+        def square_gate(c, h, pair):
+            acc = bank("z", GATE_BANK[PLAIN_BLOCKS + pair])
+            gt[pair] = held("square_gt%d" % pair, [P, JC], F32)
+            picked = slice(NH * pair, NH * (pair + 1))
+            for half in range(2):
+                t = 2 * h + half
+                for a in range(2):
+                    nc.tensor.matmul_mx(
+                        out=acc[:, NH * half : NH * (half + 1)],
+                        lhsT=zt_sb[h][:, a, :].bitcast(U8)[:, 2 * M * half : 2 * M * (half + 1)].bitcast(FP4X4),
+                        lhsT_scale=w_planes[:, 2 + a, :].bitcast(U8)[:, M * t : M * (t + 1)],
+                        rhs=t_part[c][:, a, 2 * NH * pair : 2 * NH * (pair + 1)].bitcast(FP4X4),
+                        rhs_scale=t_planes[:, a, :].bitcast(U8)[:, JC * c + NH * pair : JC * c + NH * (pair + 1)],
+                        start=a == 0,
+                        stop=False,
+                    )
+                nc.tensor.matmul_mx(
+                    out=acc[:, NH * half : NH * (half + 1)],
+                    lhsT=zv_sb[h][:, M * half : M * (half + 1)].bitcast(FP8X4),
+                    lhsT_scale=w_planes[:, 1, :].bitcast(U8)[:, M * t : M * (t + 1)],
+                    rhs=v_got[c][:, picked].bitcast(FP8X4),
+                    rhs_scale=v_plane[V_SHIFT:, JC * c + NH * pair : JC * c + NH * (pair + 1)],
+                    start=False,
+                    stop=True,
+                )
+            for half in range(2):
+                cols = slice(NH * half, NH * (half + 1))
+                t = 2 * h + half
+                nc.scalar.activation(
+                    out=gt[pair][:, cols], in_=acc[:, cols], func=TANH, bias=half_b[:, t : t + 1], scale=0.5
                 )
 
-        def turn_text(k, half):
-            back[k] = bank("minus_at_back", BACK_BANK[half])
-            for u in range(JC // M):
-                nc.tensor.transpose(
-                    back[k][:, M * u : M * (u + 1)], minus_at[u // 2][:, u % 2, M * half : M * (half + 1)], identity[:]
+        def turn(acc, source, opens, closes):
+            spots = [(half, side) for half in range(2) for side in range(2)]
+            for spot, (half, side) in enumerate(spots):
+                nc.tensor.matmul(
+                    acc[:, M * spot : M * (spot + 1)], source[:, side, M * half : M * (half + 1)], identity[:],
+                    start=opens and (closes or spot == 0), stop=closes and (opens or spot == len(spots) - 1),
+                    is_transpose=True,
+                )
+
+        def weigh_square(pair, parts):
+            mixed[pair] = held("square_mixed%d" % pair, [P, JC], F32)
+            for first, last in parts:
+                cols = slice(first, last)
+                nc.vector.scalar_tensor_tensor(
+                    out=mixed[pair][:, cols], in0=gt[pair][:, cols], scalar=1.0, in1=diff[pair][:, cols],
+                    op0=ALU.add, op1=ALU.mult,
+                )
+
+        def finish_square(c, h, pair, parts):
+            result = held("square_result%d" % pair, [P, JC], F32)
+            target = out[NH * h : NH * (h + 1), JC * c + NH * pair : JC * c + NH * (pair + 1)]
+            target = target.rearrange("(t p) j -> p t j", p=P)
+            for first, last in parts:
+                cols = slice(first, last)
+                nc.vector.scalar_tensor_tensor(
+                    out=result[:, cols], in0=mixed[pair][:, cols], scalar=0.5, in1=back[pair][:, cols],
+                    op0=ALU.mult, op1=ALU.subtract,
+                )
+                nc.sync.dma_start(
+                    out=target[:, first // NH : last // NH, :],
+                    in_=result[:, cols].rearrange("p (t j) -> p t j", j=NH),
                 )
 
         def subtract(k):
@@ -345,6 +394,7 @@ def tile_list_gmu_tanh_none_kernel(
             text_branch(*k, (0, 1))
         for k in blocks[:EARLY_GATES]:
             open_gate(*k)
+        cast(nc.vector.tensor_copy, pieces[2])
         whole = [(0, JC)]
         halves = [(0, JC // 2), (JC // 2, JC)]
         for s in range(PLAIN_BLOCKS):
@@ -359,28 +409,30 @@ def tile_list_gmu_tanh_none_kernel(
             if 1 <= s < PLAIN_BLOCKS - 1:
                 weigh(blocks[s - 1])
             subtract(blocks[s])
-            if s == 1:
-                cast(nc.vector.tensor_copy, pieces[2])
             if 1 <= s < PLAIN_BLOCKS - 1:
                 finish(blocks[s - 1], at[blocks[s - 1]], ALU.add, whole)
-        turned = blocks[PLAIN_BLOCKS:]
-        for pair in range(2):
-            turned_text(1, 1, pair)
-        for pair in range(2):
-            turned_picture(1, 1, pair)
-        for k in turned:
-            gate_branch(*k)
-        for half, k in enumerate(turned):
-            turn_into_difference(k, half, minus_at, True)
-        turn_text(turned[0], 0)
-        for half, k in enumerate(turned):
-            turn_into_difference(k, half, turned_av, False)
-        turn_text(turned[1], 1)
-        for k in blocks[PLAIN_BLOCKS - 2 : PLAIN_BLOCKS]:
-            weigh(k)
-        for k in blocks[PLAIN_BLOCKS - 2 : PLAIN_BLOCKS]:
-            finish(k, at[k], ALU.add, whole)
-        for k in turned:
-            weigh(k)
-        finish(turned[0], back[turned[0]], ALU.subtract, whole)
-        finish(turned[1], back[turned[1]], ALU.subtract, halves)
+        fifth, sixth = blocks[PLAIN_BLOCKS - 2 : PLAIN_BLOCKS]
+        turned_text(1, 1, 0)
+        turned_picture(1, 1, 0)
+        square_gate(1, 1, 0)
+        turned_text(1, 1, 1)
+        turned_picture(1, 1, 1)
+        diff[0] = bank("diff_sum", DIFF_BANK[0])
+        turn(diff[0], minus_at[0], True, False)
+        turn(diff[0], turned_av[0], False, True)
+        square_gate(1, 1, 1)
+        back[0] = bank("minus_at_back", BACK_BANK[0])
+        turn(back[0], minus_at[0], True, True)
+        diff[1] = bank("diff_sum", DIFF_BANK[1])
+        turn(diff[1], minus_at[1], True, False)
+        turn(diff[1], turned_av[1], False, True)
+        back[1] = bank("minus_at_back", BACK_BANK[1])
+        turn(back[1], minus_at[1], True, True)
+        weigh(fifth)
+        weigh(sixth)
+        finish(fifth, at[fifth], ALU.add, whole)
+        weigh_square(0, whole)
+        finish(sixth, at[sixth], ALU.add, whole)
+        finish_square(1, 1, 0, whole)
+        weigh_square(1, halves)
+        finish_square(1, 1, 1, halves)

@@ -130,7 +130,7 @@ def tile_list_gmu_tanh_none_kernel(
             nc.sync.dma_start(out=s2_win[a:32:2, :], in_=rows)
         nc.sync.dma_start(list1[:], offs)
         nc.sync.dma_start(out=w2_win[:], in_=words(tab2_words))
-        load_plane(nc.sync, s1_win, tab_scales, V_SHIFT, (0, 1))
+        load_plane(nc.sync, s1_win, tab_scales, V_SHIFT, (0, 1, 2))
         load_weight_scales(nc.sync, 2, zt_scales)
         load_weight_scales(nc.sync, 0, wv_scales)
         load_weight_scales(nc.gpsimd, 1, zv_scales)
@@ -139,7 +139,7 @@ def tile_list_gmu_tanh_none_kernel(
 
         nc.vector.tensor_copy(out=s2_got[:].bitcast(U8), in_=s2_win[:].bitcast(U8).indirect(list2[:]))
         move_t_scales()
-        load_plane(nc.sync, s1_win, tab_scales, V_SHIFT, (2, 3))
+        load_plane(nc.sync, s1_win, tab_scales, V_SHIFT, (3,))
         b_sb = shared("b_sb", "early", [P, N_TILES], F32)
         with nc.allow_non_contiguous_dma(reason="one bias value for each partition"):
             nc.gpsimd.dma_start(out=b_sb[:], in_=b.rearrange("(c p) -> p c", p=P))
@@ -157,8 +157,8 @@ def tile_list_gmu_tanh_none_kernel(
             nc.sync.dma_start(out=wv_sb[h][:], in_=words(wv_words)[:, cols])
             nc.sync.dma_start(out=zv_sb[h][:], in_=words(zv_words)[:, cols])
 
-        nc.sync.dma_start(out=w1_win[:], in_=words(tab_words))
         load_zt(0)
+        nc.sync.dma_start(out=w1_win[:], in_=words(tab_words))
         for r in range(ROWS):
             nc.sync.dma_start(
                 out=w_planes[r:P:32, :, :], in_=w_planes[STAGE + r : STAGE + QUADS * ROWS : ROWS, :, :]

from contextlib import ExitStack

import concourse.mybir as mybir
from concourse.masks import make_identity

K, L, N, T, J = 512, 1024, 512, 2048, 1024
FLOPS = 2 * 2 * (K + L) * N * J

F32 = mybir.dt.float32
BF16 = mybir.dt.bfloat16
I32 = mybir.dt.int32
U32 = mybir.dt.uint32
U16 = mybir.dt.uint16
U8 = mybir.dt.uint8
FP8X4 = mybir.dt.float8_e4m3fn_x4
FP4X4 = mybir.dt.float4_e2m1fn_x4
ALU = mybir.AluOpType
TANH = mybir.ActivationFunctionType.Tanh

P = 128
PACK = 4
QUADS = 4
ROWS = 4
M = 128
N_TILES = N // M
JC = 512
J_CHUNKS = J // JC
NH = 256
V_SHIFT = 4
EARLY = 4
PLAIN_BLOCKS = 6
EARLY_GATES = 3
TEXT_BANK = (0, 1, 2, 3, 5, 0, 7, 6)
PICTURE_BANK = (4, 6, 5, 7, 4, 2, 5, 4)
GATE_BANK = (5, 7, 0, 6, 1, 3, 1, 0)
DIFF_BANK = (2, 7)
BACK_BANK = (3, 5)
STAGE = 16
WARM_UP_PASSES = 4
WARM_UP_BANK = 4


def tile_list_gmu_tanh_none_kernel(
    tc, tab_words, tab_scales, tab2_words, tab2_scales, zv_words, zv_scales, zt_words, zt_scales, b,
    wv_words, wv_scales, wt, offs, offs2, out
):
    nc = tc.nc
    with ExitStack() as ctx:
        keep = ctx.enter_context(tc.tile_pool(name="keep", bufs=1))
        work = ctx.enter_context(tc.tile_pool(name="work", bufs=3))
        psum = ctx.enter_context(tc.psum_pool(name="psum", bufs=1))

        def held(name, shape, dtype):
            return keep.tile(shape, dtype, name=name, align_bytes=64)

        def shared(name, tag, shape, dtype):
            return keep.tile(shape, dtype, name=name, tag=tag, align_bytes=64)

        list1 = keep.tile([P, J // 16], U16, name="list1")
        list2 = keep.tile([P, J // 16], U16, name="list2")
        s1_win = held("s1_win", [P, T // 4], I32)
        s2_win = shared("s2_win", "early", [P, T // 4], I32)
        s2_got = held("s2_got", [P, J // 4], I32)
        t_planes = held("t_planes", [P, 2, J // 4], I32)
        w_planes = held("w_planes", [P, 4, N // 4], I32)
        w1_win = held("w1_win", [P, T], I32)
        wv_sb = [held("wv_sb%d" % h, [P, NH], I32) for h in range(N // NH)]
        zv_sb = [held("zv_sb%d" % h, [P, NH], I32) for h in range(N // NH)]
        zt_sb = [held("zt_sb%d" % h, [P, 2, NH // 2], I32) for h in range(N // NH)]
        w2_win = held("w2_win", [P, T], I32)
        wt_codes = held("wt_codes", [P, 2, N], U32)
        wt_plane = held("wt_plane", [P, 2, N], U8)
        pieces = [(a, h) for h in range(N // NH) for a in range(2)]
        wt_raw, wt_bf = {}, {}
        v_got = [held("v_got%d" % c, [P, JC], U32) for c in range(J_CHUNKS)]
        t_got = [held("t_got%d" % c, [P, JC], U32) for c in range(J_CHUNKS)]
        t_part = {}

        nc.gpsimd.memset(s1_win[:], 0)
        nc.gpsimd.memset(w_planes[:], 0)
        nc.vector.memset(s2_win[32:64, :], 0)
        nc.vector.memset(s2_win[64:128, :], 0)
        nc.gpsimd.memset(t_planes[:], 0)
        identity = held("identity", [P, P], F32)
        make_identity(nc, identity[:])

        def load_wt(k):
            a, h = k
            wt_raw[k] = shared("wt_raw%d%d" % k, "raw%d%d" % k, [P, PACK, NH], F32)
            rows = wt[512 * a : 512 * (a + 1), NH * h : NH * (h + 1)]
            nc.sync.dma_start(out=wt_raw[k][:], in_=rows.rearrange("(p i) n -> p i n", i=PACK))

        def words(ap):
            return ap[0].rearrange("p n i -> p (n i)").bitcast(I32)

        def cast(copy, k):
            wt_bf[k] = shared("wt_bf%d%d" % k, "wt_bf%d%d" % k, [P, NH, PACK], BF16)
            copy(
                out=wt_bf[k][:].rearrange("p (c n) i -> p c i n", n=4),
                in_=wt_raw[k][:].rearrange("p i (c n) -> p c i n", n=4),
            )

        def quantise(k):
            a, h = k
            cols = slice(NH * h, NH * (h + 1))
            nc.vector.quantize_mx(
                out=wt_codes[:, a, cols].bitcast(FP8X4),
                scales=wt_plane[:, a, cols],
                in_=wt_bf[k][:].rearrange("p n i -> p (n i)"),
            )

        def move_t_scales():
            for r in range(ROWS):
                rows = s2_got[2 * QUADS * r : 2 * QUADS * (r + 1), :]
                nc.sync.dma_start(out=t_planes[r:P:32, :, :], in_=rows)

        def load_plane(queue, plane, scales, shift, which):
            for r in which:
                rows = scales[0, r::ROWS, :]
                queue.dma_start(out=plane[shift + r : P : 32, :], in_=rows.bitcast(I32))

        def load_weight_scales(queue, first, scales):
            passes = scales.shape[0]
            rows = scales.rearrange("a q n -> q a n").bitcast(I32)
            queue.dma_start(out=w_planes[STAGE : STAGE + QUADS * ROWS, first : first + passes, :], in_=rows)

        nc.sync.dma_start(list2[:], offs2)
        for a in range(2):
            rows = tab2_scales[a].rearrange("(q r) t -> r q t", r=ROWS).bitcast(I32)
            nc.sync.dma_start(out=s2_win[a:32:2, :], in_=rows)
        nc.sync.dma_start(list1[:], offs)
        nc.sync.dma_start(out=w2_win[:], in_=words(tab2_words))
        load_plane(nc.sync, s1_win, tab_scales, V_SHIFT, (0, 1, 2))
        load_weight_scales(nc.sync, 2, zt_scales)
        load_weight_scales(nc.sync, 0, wv_scales)
        load_weight_scales(nc.gpsimd, 1, zv_scales)
        for k in pieces[:2]:
            load_wt(k)

        nc.vector.tensor_copy(out=s2_got[:].bitcast(U8), in_=s2_win[:].bitcast(U8).indirect(list2[:]))
        move_t_scales()
        load_plane(nc.sync, s1_win, tab_scales, V_SHIFT, (3,))
        b_sb = shared("b_sb", "early", [P, N_TILES], F32)
        with nc.allow_non_contiguous_dma(reason="one bias value for each partition"):
            nc.gpsimd.dma_start(out=b_sb[:], in_=b.rearrange("(c p) -> p c", p=P))
        half_b = held("half_b", [P, N_TILES], F32)
        nc.gpsimd.tensor_scalar(
            out=half_b[:], in0=b_sb[:], scalar1=0.5, scalar2=0.0, op0=ALU.mult, op1=ALU.add
        )

        def load_zt(h):
            halves = slice(NH // 2 * h, NH // 2 * (h + 1))
            nc.sync.dma_start(out=zt_sb[h][:], in_=zt_words.rearrange("a p n -> p a n").bitcast(I32)[:, :, halves])

        def load_v_weights(h):
            cols = slice(NH * h, NH * (h + 1))
            nc.sync.dma_start(out=wv_sb[h][:], in_=words(wv_words)[:, cols])
            nc.sync.dma_start(out=zv_sb[h][:], in_=words(zv_words)[:, cols])

        load_zt(0)
        nc.sync.dma_start(out=w1_win[:], in_=words(tab_words))
        for r in range(ROWS):
            nc.sync.dma_start(
                out=w_planes[r:P:32, :, :], in_=w_planes[STAGE + r : STAGE + QUADS * ROWS : ROWS, :, :]
            )
        load_v_weights(0)
        load_wt(pieces[2])
        load_wt(pieces[3])
        load_zt(1)
        load_v_weights(1)

        def entries(lst, c):
            return lst[:, c * JC // 16 : (c + 1) * JC // 16]

        def gather_t(c):
            nc.vector.tensor_copy(out=t_got[c][:], in_=w2_win[:].bitcast(U32).indirect(entries(list2, c)))

        def part_t(c, tag):
            t_part[c] = shared("t_part%d" % c, tag, [P, 2, 2 * JC], U8)
            nc.vector.tensor_copy(
                out=t_part[c][:].bitcast(U16), in_=t_got[c][:].bitcast(U16).rearrange("p (j d) -> p d j", d=2)
            )

        def gather_v(c):
            nc.vector.tensor_copy(out=v_got[c][:], in_=w1_win[:].bitcast(U32).indirect(entries(list1, c)))

        def v_pass(acc, weights, plane, c, t, start, stop):
            nc.tensor.matmul_mx(
                out=acc[:],
                lhsT=weights[t // 2][:, M * (t % 2) : M * (t % 2 + 1)].bitcast(FP8X4),
                lhsT_scale=w_planes[:, plane, :].bitcast(U8)[:, M * t : M * (t + 1)],
                rhs=v_got[c][:].bitcast(FP8X4),
                rhs_scale=v_plane[V_SHIFT:, JC * c : JC * (c + 1)],
                start=start,
                stop=stop,
            )

        def t_pass(acc, lhsT, lhsT_scale, c, a, start, stop):
            nc.tensor.matmul_mx(
                out=acc[:],
                lhsT=lhsT,
                lhsT_scale=lhsT_scale,
                rhs=t_part[c][:, a, :].bitcast(FP4X4),
                rhs_scale=t_planes[:, a, :].bitcast(U8)[:, JC * c : JC * (c + 1)],
                start=start,
                stop=stop,
            )

        at, av, gt, diff, mixed, z_sum = {}, {}, {}, {}, {}, {}

        def bank(name, number):
            return psum.tile([P, JC], F32, name=name, tag="bank%d" % number)

        def text_branch(c, t, order):
            acc = bank("ht", TEXT_BANK[blocks.index((c, t))])
            cols = slice(M * t, M * (t + 1))
            for a in order:
                codes = wt_codes[:, a, cols].bitcast(FP8X4)
                t_pass(acc, codes, wt_plane[:, a, cols], c, a, a == order[0], a == order[1])
            if (c, t) not in at:
                at[c, t] = held("at%d%d" % (c, t), [P, JC], F32)[:]
            nc.scalar.activation(out=at[c, t], in_=acc[:], func=TANH)

        def picture_branch(c, t):
            acc = bank("hv", PICTURE_BANK[blocks.index((c, t))])
            v_pass(acc, wv_sb, 0, c, t, True, True)
            av[c, t] = held("av%d%d" % (c, t), [P, JC], F32)
            nc.scalar.activation(out=av[c, t][:], in_=acc[:], func=TANH)

        def open_gate(c, t):
            acc = z_sum[c, t] = bank("z", GATE_BANK[blocks.index((c, t))])
            for a in range(2):
                codes = zt_sb[t // 2][:, a, :].bitcast(U8)[:, 2 * M * (t % 2) : 2 * M * (t % 2 + 1)].bitcast(FP4X4)
                scale = w_planes[:, 2 + a, :].bitcast(U8)[:, M * t : M * (t + 1)]
                t_pass(acc, codes, scale, c, a, a == 0, False)

        def gate_branch(c, t):
            if (c, t) not in z_sum:
                open_gate(c, t)
            acc = z_sum[c, t]
            v_pass(acc, zv_sb, 1, c, t, False, True)
            gt[c, t] = held("gt%d%d" % (c, t), [P, JC], F32)
            nc.scalar.activation(out=gt[c, t][:], in_=acc[:], func=TANH, bias=half_b[:, t : t + 1], scale=0.5)

        def turned_text(c, h, pair):
            acc = bank("ht", TEXT_BANK[PLAIN_BLOCKS + pair])
            for side in range(2):
                u = 2 * pair + side
                for a in (1, 0):
                    nc.tensor.matmul_mx(
                        out=acc[:, NH * side : NH * (side + 1)],
                        lhsT=t_part[c][:, a, 2 * M * u : 2 * M * (u + 1)].bitcast(FP4X4),
                        lhsT_scale=t_planes[:, a, :].bitcast(U8)[:, JC * c + M * u : JC * c + M * (u + 1)],
                        rhs=wt_codes[:, a, NH * h : NH * (h + 1)].bitcast(FP8X4),
                        rhs_scale=wt_plane[:, a, NH * h : NH * (h + 1)],
                        start=a == 1,
                        stop=a == 0,
                    )
            minus_at[pair] = held("minus_at%d" % pair, [P, 2, NH], F32)
            nc.scalar.activation(
                out=minus_at[pair][:].rearrange("p s n -> p (s n)"), in_=acc[:], func=TANH, scale=-1.0
            )

        def turned_picture(c, h, pair):
            acc = bank("hv", PICTURE_BANK[PLAIN_BLOCKS + pair])
            for side in range(2):
                u = 2 * pair + side
                nc.tensor.matmul_mx(
                    out=acc[:, NH * side : NH * (side + 1)],
                    lhsT=v_got[c][:, M * u : M * (u + 1)].bitcast(FP8X4),
                    lhsT_scale=v_plane[V_SHIFT:, JC * c + M * u : JC * c + M * (u + 1)],
                    rhs=wv_sb[h][:].bitcast(FP8X4),
                    rhs_scale=w_planes[:, 0, :].bitcast(U8)[:, NH * h : NH * (h + 1)],
                    start=True,
                    stop=True,
                )
            turned_av[pair] = held("turned_av%d" % pair, [P, 2, NH], F32)
            nc.scalar.activation(out=turned_av[pair][:].rearrange("p s n -> p (s n)"), in_=acc[:], func=TANH)

        def square_gate(c, h, pair):
            acc = bank("z", GATE_BANK[PLAIN_BLOCKS + pair])
            gt[pair] = held("square_gt%d" % pair, [P, JC], F32)
            picked = slice(NH * pair, NH * (pair + 1))
            for half in range(2):
                t = 2 * h + half
                for a in range(2):
                    nc.tensor.matmul_mx(
                        out=acc[:, NH * half : NH * (half + 1)],
                        lhsT=zt_sb[h][:, a, :].bitcast(U8)[:, 2 * M * half : 2 * M * (half + 1)].bitcast(FP4X4),
                        lhsT_scale=w_planes[:, 2 + a, :].bitcast(U8)[:, M * t : M * (t + 1)],
                        rhs=t_part[c][:, a, 2 * NH * pair : 2 * NH * (pair + 1)].bitcast(FP4X4),
                        rhs_scale=t_planes[:, a, :].bitcast(U8)[:, JC * c + NH * pair : JC * c + NH * (pair + 1)],
                        start=a == 0,
                        stop=False,
                    )
                nc.tensor.matmul_mx(
                    out=acc[:, NH * half : NH * (half + 1)],
                    lhsT=zv_sb[h][:, M * half : M * (half + 1)].bitcast(FP8X4),
                    lhsT_scale=w_planes[:, 1, :].bitcast(U8)[:, M * t : M * (t + 1)],
                    rhs=v_got[c][:, picked].bitcast(FP8X4),
                    rhs_scale=v_plane[V_SHIFT:, JC * c + NH * pair : JC * c + NH * (pair + 1)],
                    start=False,
                    stop=True,
                )
            for half in range(2):
                cols = slice(NH * half, NH * (half + 1))
                t = 2 * h + half
                nc.scalar.activation(
                    out=gt[pair][:, cols], in_=acc[:, cols], func=TANH, bias=half_b[:, t : t + 1], scale=0.5
                )

        def turn(acc, source, opens, closes):
            spots = [(half, side) for half in range(2) for side in range(2)]
            for spot, (half, side) in enumerate(spots):
                nc.tensor.matmul(
                    acc[:, M * spot : M * (spot + 1)], source[:, side, M * half : M * (half + 1)], identity[:],
                    start=opens and (closes or spot == 0), stop=closes and (opens or spot == len(spots) - 1),
                    is_transpose=True,
                )

        def weigh_square(pair, parts):
            mixed[pair] = held("square_mixed%d" % pair, [P, JC], F32)
            for first, last in parts:
                cols = slice(first, last)
                nc.vector.scalar_tensor_tensor(
                    out=mixed[pair][:, cols], in0=gt[pair][:, cols], scalar=1.0, in1=diff[pair][:, cols],
                    op0=ALU.add, op1=ALU.mult,
                )

        def finish_square(c, h, pair, parts):
            result = held("square_result%d" % pair, [P, JC], F32)
            target = out[NH * h : NH * (h + 1), JC * c + NH * pair : JC * c + NH * (pair + 1)]
            target = target.rearrange("(t p) j -> p t j", p=P)
            for first, last in parts:
                cols = slice(first, last)
                nc.vector.scalar_tensor_tensor(
                    out=result[:, cols], in0=mixed[pair][:, cols], scalar=0.5, in1=back[pair][:, cols],
                    op0=ALU.mult, op1=ALU.subtract,
                )
                nc.sync.dma_start(
                    out=target[:, first // NH : last // NH, :],
                    in_=result[:, cols].rearrange("p (t j) -> p t j", j=NH),
                )

        def subtract(k):
            diff[k] = work.tile([P, JC], F32, name="diff")
            nc.vector.tensor_tensor(out=diff[k][:], in0=av[k][:], in1=at[k], op=ALU.subtract)

        def weigh(k):
            mixed[k] = held("mixed%d%d" % k, [P, JC], F32)
            nc.vector.scalar_tensor_tensor(
                out=mixed[k][:], in0=gt[k][:], scalar=1.0, in1=diff[k][:], op0=ALU.add, op1=ALU.mult
            )

        def finish(k, text, op, parts):
            c, t = k
            result = held("result%d%d" % k, [P, JC], F32)
            for first, last in parts:
                cols = slice(first, last)
                nc.vector.scalar_tensor_tensor(
                    out=result[:, cols], in0=mixed[k][:, cols], scalar=0.5, in1=text[:, cols], op0=ALU.mult, op1=op
                )
                nc.sync.dma_start(out=out[M * t : M * (t + 1), JC * c + first : JC * c + last], in_=result[:, cols])

        minus_at, turned_av, back = {}, {}, {}
        for c in range(J_CHUNKS):
            gather_t(c)
        warm = bank("warm", WARM_UP_BANK)
        for repeat in range(WARM_UP_PASSES):
            nc.tensor.matmul_mx(
                out=warm[:],
                lhsT=t_got[0][:].bitcast(U8)[:, : 2 * M].bitcast(FP4X4),
                lhsT_scale=s2_got[:].bitcast(U8)[:, :M],
                rhs=t_got[0][:].bitcast(U8)[:, : 2 * JC].bitcast(FP4X4),
                rhs_scale=s2_got[:].bitcast(U8)[:, :JC],
                start=True,
                stop=True,
            )
        part_t(0, "t_part0")
        cast(nc.scalar.copy, pieces[0])
        quantise(pieces[0])
        part_t(1, "raw%d%d" % pieces[0])
        cast(nc.scalar.copy, pieces[1])
        quantise(pieces[1])
        v_plane = shared("v_plane", "raw%d%d" % pieces[1], [P, J], U8)
        nc.vector.tensor_copy(out=v_plane[:], in_=s1_win[:].bitcast(U8).indirect(list1[:]))
        gather_v(0)
        gather_v(1)
        blocks = [(c, 2 * h + t) for h in range(2) for c in range(J_CHUNKS) for t in range(2)]

        at_early = held("at_early", [P, EARLY, JC], F32)
        for s, k in enumerate(blocks[:EARLY]):
            at[k] = at_early[:, s, :]
            text_branch(*k, (0, 1))
        for k in blocks[:EARLY_GATES]:
            open_gate(*k)
        cast(nc.vector.tensor_copy, pieces[2])
        whole = [(0, JC)]
        halves = [(0, JC // 2), (JC // 2, JC)]
        for s in range(PLAIN_BLOCKS):
            if s == 2:
                cast(nc.scalar.copy, pieces[3])
                quantise(pieces[2])
                quantise(pieces[3])
            if s >= EARLY:
                text_branch(*blocks[s], (1, 0))
            picture_branch(*blocks[s])
            gate_branch(*blocks[s])
            if 1 <= s < PLAIN_BLOCKS - 1:
                weigh(blocks[s - 1])
            subtract(blocks[s])
            if 1 <= s < PLAIN_BLOCKS - 1:
                finish(blocks[s - 1], at[blocks[s - 1]], ALU.add, whole)
        fifth, sixth = blocks[PLAIN_BLOCKS - 2 : PLAIN_BLOCKS]
        turned_text(1, 1, 0)
        turned_picture(1, 1, 0)
        square_gate(1, 1, 0)
        turned_text(1, 1, 1)
        turned_picture(1, 1, 1)
        diff[0] = bank("diff_sum", DIFF_BANK[0])
        turn(diff[0], minus_at[0], True, False)
        turn(diff[0], turned_av[0], False, True)
        square_gate(1, 1, 1)
        back[0] = bank("minus_at_back", BACK_BANK[0])
        turn(back[0], minus_at[0], True, True)
        diff[1] = bank("diff_sum", DIFF_BANK[1])
        turn(diff[1], minus_at[1], True, False)
        turn(diff[1], turned_av[1], False, True)
        back[1] = bank("minus_at_back", BACK_BANK[1])
        turn(back[1], minus_at[1], True, True)
        weigh(fifth)
        weigh(sixth)
        finish(fifth, at[fifth], ALU.add, whole)
        weigh_square(0, whole)
        finish(sixth, at[sixth], ALU.add, whole)
        finish_square(1, 1, 0, whole)
        weigh_square(1, halves)
        finish_square(1, 1, 1, halves)
